import numpy as np, ml_dtypes
CORES = [2,3,42,43,82,83,122,123]
N = 8
BF = ml_dtypes.bfloat16
W, B, L, J, VIS, ST = 3584, 2560, 128, 1024, 4, 3
def pick(rng, share, *tail):
    v = rng.integers(0, W, (N, 8) + tail); pool = rng.integers(0, W, (N, 8, 64)); ix = rng.integers(0, 64, (N, 8) + tail)
    h = np.take_along_axis(pool, ix.reshape(N, 8, -1), 2).reshape(v.shape)
    return np.where(rng.random(v.shape) < np.reshape(share, (N, 8) + (1,) * len(tail)), h, v)
def thread(rng, par, share, out):
    ft = np.full((N, 8, J), W, np.int64); a = np.arange(N)[:, None]; g = np.arange(8)[None, :]
    order = B + np.argsort(rng.random((N, 8, J)), axis=-1)
    for s in range(J):
        n = order[:, :, s]; base = rng.integers(0, B, (N, 8)); o = rng.random((N, 8)) < out
        x = np.where(rng.random((N, 8)) < (share if s else 0.0), order[a, g, rng.integers(0, max(s, 1), (N, 8))], base)
        up = par[a, g, x]
        par[a, g, n] = np.where(o, base, up); par[a, g, x] = np.where(o, up, n); ft[a, g, n - B] = np.where(o, W, x)
        v = np.maximum(up - B, 0); cur = ft[a, g, v]
        ft[a, g, v] = np.where(~o & (up >= B) & (cur == x), n, cur)
    return ft
def parts(rng):
    sh = np.array([0.05, 0.1, 0.3, 0.5])
    x = rng.integers(0, 256, (N, 8, 16, W)); kn = np.zeros((N, 8, 16, W), np.int64)
    kn[:, :, 1:] = pick(rng, rng.choice(sh, (N, 8)), 15, W)
    par = np.zeros((N, 8, W), np.int64); par[:, :, :B] = (rng.random((N, 8, B)) * np.arange(B)).astype(np.int64)
    ft = thread(rng, par, rng.choice(np.array([0.2, 0.5, 0.8]), (N, 8)), 0.0625); kn[:, :, 0] = par
    tr = pick(rng, rng.choice(sh, (N, 8)), W); b = pick(rng, rng.choice(sh, (N, 8)), L); z = rng.integers(0, 256, (N, 8, 16, L))
    m = rng.random((N, 8, L)) < 0.08
    oj = B + L * np.arange(N)[:, None, None] + rng.integers(0, L, (N, 8, L))
    near = np.take_along_axis(x, oj[:, :, None, :], 3) + rng.integers(-9, 10, z.shape)
    b = np.where(m, oj, b); z = np.where(m[:, :, None, :], np.minimum(np.maximum(near, 0), 255), z)
    return x, kn, tr, ft, z, b
def pack(x, kn, tr, ft, z, b):
    return {"x0": np.ascontiguousarray(x.reshape(N, 128, W)).astype(np.float32).astype(BF), "kn": np.ascontiguousarray(kn.reshape(N, 128, W)).astype(np.int32), "tr": tr.astype(np.int32),
            "ft": ft.astype(np.int32), "z0": np.ascontiguousarray(z.reshape(N, 128, L)).astype(np.float32).astype(BF), "bs": b.astype(np.int32)}
def setup_inputs(rng):
    return pack(*parts(rng))
def uneven(rng, top, p, *shape):
    return np.minimum((top * rng.random(shape) ** p).astype(np.int64), top - 1)
def setup_inputs_spread(rng):
    x, kn, tr, ft, z, b = parts(rng); ps = np.array([0.25, 0.5, 1.0, 2.0, 4.0, 8.0])
    x = uneven(rng, 256, rng.choice(ps, (N, 8, 1, W)), N, 8, 16, W); z = uneven(rng, 256, rng.choice(ps, (N, 8, 1, L)), N, 8, 16, L)
    k2 = uneven(rng, W, rng.choice(ps, (N, 8, 16, 1)), N, 8, 16, W); kn[:, :, 1:] = k2[:, :, 1:]; kn[:, 1::2, 0] = k2[:, 1::2, 0]
    f2 = uneven(rng, W + 1, rng.choice(ps, (N, 8, 1)), N, 8, J); ft[:, 1::2] = f2[:, 1::2]
    tr = uneven(rng, W, rng.choice(ps, (N, 8, 1)), N, 8, W); b = uneven(rng, W, rng.choice(ps, (N, 8, 1)), N, 8, L)
    return pack(x, kn, tr, ft, z, b)
def two(rng, lo, hi, *shape):
    return np.where(rng.random(shape) < 0.5, lo, hi)
def setup_inputs_ends(rng):
    x, kn, tr, ft, z, b = parts(rng); e = np.array([0, W - 1])
    x = np.where(rng.random((N, 8, 1, W)) < 0.5, two(rng, 0, 255, N, 8, 1, W), two(rng, 0, 255, N, 8, 16, W))
    z = np.where(rng.random((N, 8, 1, L)) < 0.6, two(rng, 0, 255, N, 8, 1, L), two(rng, 0, 255, N, 8, 16, L))
    kn = np.where(rng.random((N, 8, 16, W)) < 0.72, two(rng, 0, W - 1, N, 8, 16, W), kn)
    tr = np.where(rng.random((N, 8, W)) < 0.7, two(rng, 0, W - 1, N, 8, W), tr)
    ft = np.where(rng.random((N, 8, J)) < 0.7, two(rng, 0, W, N, 8, J), ft)
    b = np.where(rng.random((N, 8, L)) < 0.7, two(rng, 0, W - 1, N, 8, L), b)
    s = int(rng.integers(0, 4))
    for q in range(N):
        for g in range(8):
            c = (q + g + s) % 4
            x[q, g, :, 0] = 255 * (c & 1); x[q, g, :, W - 1] = 255 * (c >> 1)
        v = 255 * ((q + s) & 1); w = (q >> 1) & 1
        x[q, 7, :, 0] = v; x[q, 7, :, W - 1] = v
        kn[q, 7][:, e] = two(rng, 0, W - 1, 16, 2); kn[q, 7, 14, e] = 0; kn[q, 7, 15, e] = W - 1
        z[q, 7, :, w::2] = 255 - v; z[q, 7, :, 1 - w::2] = v
        b[q, 7, :] = two(rng, 0, W - 1, L); b[q, 7, L - 2:] = W - 1
        z[q, :, :, L - 1] = np.where(np.arange(8)[:, None] % 2 == q % 2, 0, 255)
        lo = B + L * ((q - 1) % N)
        x[q, 6] = 255 * (q & 1); z[q, 6] = 255 * (q & 1); tr[q, 6] = 0
        kn[q, 6, :, 0] = rng.integers(lo, lo + L, 16); b[q, 6] = np.where(b[q, 6] == 0, W - 1, b[q, 6])
    return pack(x, kn, tr, ft, z, b)
def chain(par, fo, seq, x):
    up = int(par[x]); par[x] = seq[0]; fo[seq[0] - B] = x
    par[seq[:-1]] = seq[1:]; fo[seq[1:] - B] = seq[:-1]; par[seq[-1]] = up
def setup_inputs_corners(rng):
    x, kn, tr, ft, z, b = parts(rng); sh = int(rng.integers(0, 8)); jn = B + np.arange(J); sits = []
    kinj = B + L * rng.integers(0, N, (N, 8, 1, W)) + rng.integers(0, L, (N, 8, 15, W))
    kn[:, :, 1:] = np.where(rng.random((N, 8, 1, W)) < 0.15, kinj, kn[:, :, 1:])
    for q in range(N):
        nx = L * ((q + 1) % N)
        for g in range(8):
            c = (q + g + sh) % 8; par = kn[q, g, 0]; fo = ft[q, g]
            if c == 7: continue
            par[:] = rng.integers(0, B, W); fo[:] = W; p = rng.permutation(B)[:J]
            if c == 0:
                m = rng.random(W) < 0.1; kn[q, g][:, m] = B + L * rng.integers(0, N, (1, W))[:, m] + rng.integers(0, L, (16, W))[:, m]
            if c == 1: chain(par, fo, jn, int(rng.integers(0, B)))
            if c == 2: chain(par, fo, np.ascontiguousarray(jn.reshape(N, L).T).reshape(-1), int(rng.integers(0, B)))
            if c == 3:
                up = par[p].copy(); par[p] = jn; fo[:] = p; par[B:] = up
                if q % 2 == 0: sits.append((q, g, np.arange(L), p[nx:nx + L]))
            if c == 4:
                fo[:] = rng.integers(0, W + 1, J); par[B:] = rng.integers(0, W, J)
                i = int(rng.integers(0, L)); m = L * min(q, N - 2) + i
                fo[m] = W; par[B + m] = rng.integers(0, B); par[W - 1] = B + m
                if q > 0:
                    n = L * q + (i + 1) % (L - 1); y = int(rng.integers(1, B))
                    fo[n] = y; par[y] = B + n; par[B + n] = rng.integers(0, B)
                    fo[0] = B + n; par[B] = B + 1; fo[1] = W; x[q, g, :, B] = 255 * (np.arange(16) % 2)
            if c == 5:
                fo[:] = 0; par[0] = B + rng.integers(0, J); par[B:] = two(rng, 0, B - 1, J)
            if c == 6:
                w = np.arange(J) % 3
                fo[:] = np.where(w == 0, jn, np.where(w == 1, W, p)); par[p[w == 2]] = jn[w == 2]
                par[B:] = np.where(w == 1, jn, np.where(w == 2, B + (np.arange(J) + L) % J, par[B:]))
                ls = rng.permutation(np.nonzero(w[L * q:L * q + L] == 2)[0])[:8]; js = B + nx + ls
                fo[js - B] = js; par[js] = js; sits.append((q, g, ls, js))
    ch = rng.integers(0, 5, (N, 8, L)); ro = B + L * np.arange(N)[:, None, None] + 0 * ch
    b = np.choose(ch, [0 * ch, 0 * ch + W - 1, ro + np.arange(L), ro + rng.integers(0, L, (N, 8, L)), b])
    h = rng.integers(0, 4, (N, 8, W)); tr = np.choose(h, [rng.integers(B, W, (N, 8, W)), two(rng, 0, W - 1, N, 8, W), tr, tr])
    for q, g, i, v in sits:
        b[q, g, i] = v; z[q, g][:, i] = x[q, g][:, v]
    return pack(x, kn, tr, ft, z, b)
def setup_inputs_crowd(rng):
    x, kn, tr, ft, z, b = parts(rng); hs = np.zeros((N, 8), np.int64)
    for q in range(N):
        own = B + L * q
        kn[q, :, 0, own:own + L] = rng.integers(0, B, (8, L)); ft[q, :, L * q:L * q + L] = W
        for g in range(8):
            h = int(rng.integers(1, B - 1)); h2 = h + 1; c = (g + q) % 4; hs[q, g] = h
            if q < 2:
                b[q, g] = h; kn[q, g, :, h] = h; kn[q, g, :, h2] = h2
                if q == 1 and g % 2: b[q, g, int(rng.integers(0, L))] = h2
            elif q == N - 1:
                b[q, g] = W - 1; kn[q, g, 1:, W - 1] = rng.integers(own, own + L, 15)
                up = int(kn[q, g, 0, W - 1]); x[q, g, :, up] = x[q, g, :, W - 1]
            elif q == 2:
                s = rng.permutation(B)[:L]; b[q, g] = s; kn[q, g][:, s] = s
            else: b[q, g] = rng.choice(np.array([0, h, h2, W - 1]), L)
            if c == 0: tr[q, g] = W - 1
            if c == 1: tr[q, g] = two(rng, 0, h, W)
            if c == 2: tr[q, g] = h
    for g in range(8):
        h = int(hs[0, g]); e = (h + 3) % B; e2 = (h + 4) % B
        kn[0, g, :, e] = e2; kn[0, g, :, e2] = e2; x[0, g, :, e2] = x[0, g, :, e]; tr[N - 1, g, W - 1] = e
    for g in (3, 7):
        h = int(hs[0, g]); e = (int(hs[1, g]) + 3) % B; js = B + rng.permutation(L)[:16]
        z[0, g] = 0; x[0, g, :, h] = 0; tr[0, g, h] = e
        x[1, g, :, e] = 255; kn[1, g, :, e] = js; x[1, g][:, js] = 0; ft[1, g, js[0] - B] = W
    return pack(x, kn, tr, ft, z, b)
def setup_inputs_ties(rng):
    x, kn, tr, ft, z, b = parts(rng)
    lo = rng.integers(0, 247, (N, 8, 1, 1)); sp = np.array([1, 2, 4, 9])[(np.arange(8)[None, :] + rng.integers(0, 4, (N, 1))) % 4].reshape(N, 8, 1, 1)
    x = lo + (rng.random((N, 8, 16, W)) * sp).astype(np.int64); z = lo + (rng.random((N, 8, 16, L)) * sp).astype(np.int64)
    x[..., 1::2] = np.where(rng.random((N, 8, 1, W // 2)) < 0.5, x[..., ::2], x[..., 1::2])
    kn[:, :, 9:] = np.where(rng.random((N, 8, 7, W)) < 0.5, kn[:, :, 2:9], kn[:, :, 9:])
    return pack(x, kn, tr, ft, z, b)
def check_inputs(d):
    bad = []
    for k, lo, hi in (("x0", 0, 255), ("kn", 0, W - 1), ("tr", 0, W - 1), ("ft", 0, W), ("z0", 0, 255), ("bs", 0, W - 1)):
        a = np.asarray(d[k]).astype(np.float64)
        if not (np.min(a) >= lo and np.max(a) <= hi): bad.append("range of " + k)
        elif np.any(np.floor(a) != a): bad.append("whole numbers in " + k)
    return bad
def own(v, r):
    return (v >= B + L * r) & (v < B + L * r + L)
def lowest(key):
    return np.argmax(key[:, :, None] == key[:, None, :], axis=2) == np.arange(L)
def reference(x0, kn, tr, ft, z0, bs):
    X = x0.astype(np.float32).astype(np.int32).reshape(N, 8, 16, W); KN = kn.astype(np.int64).reshape(N, 8, 16, W)
    TR = tr.astype(np.int64); FT = ft.astype(np.int64)
    z = z0.astype(np.float32).astype(np.int32).reshape(N, 8, 16, L); b = bs.astype(np.int64); b0 = np.zeros((N, 8, L), np.int64); A = [0] * N
    g = np.arange(8)[:, None]; lane = np.arange(L)
    for t in range(VIS):
        for q in range(N):
            r = (q - t) % N; lo = B + L * r; Xq = X[q]; Kq = KN[q]; par = Kq[:, 0]; fo = FT[q]; zz = z[r].copy(); s = b[r].copy()
            n = lo + lane; y = fo[:, L * r:L * r + L].copy(); u = par[:, lo:lo + L].copy()
            live = ~own(y, r) & ~own(u, r)
            held = live & (y < W) & (par[g, np.minimum(y, W - 1)] == n)
            uj = np.maximum(u - B, 0); turn = held & (u >= B) & (fo[g, uj] == n)
            gi, li = np.nonzero(held); par[gi, y[gi, li]] = u[gi, li]
            gi, li = np.nonzero(turn); fo[gi, uj[gi, li]] = y[gi, li]
            fo[:, L * r:L * r + L] = np.where(live, W, y)
            for step in range(ST):
                c = Kq[g, :, s]
                xc = np.take_along_axis(Xq, c.reshape(8, 1, L * 16), 2).reshape(8, 16, L, 16)
                d = np.where(own(c, r), 2 ** 20, np.add.reduce(np.abs(xc - zz[:, :, :, None]), axis=1))
                k = np.argmin(d, axis=2)[:, :, None]
                best = np.take_along_axis(d, k, 2)[:, :, 0]; cand = np.take_along_axis(c, k, 2)[:, :, 0]
                here = np.add.reduce(np.abs(np.take_along_axis(Xq, s[:, None, :], 2) - zz), axis=1)
                s = np.where(best < here + (A[r] & 31), cand, s)
            may = live & ~own(s, r); seat = may & lowest(np.where(may, s, W + lane))
            xs = np.take_along_axis(Xq, s[:, None, :], 2)
            gi, li = np.nonzero(seat); m = s[gi, li]; nn = lo + li
            cols = Kq[gi, :, m]; up = cols[:, 0].copy()
            hit = (up >= B) & (fo[gi, np.maximum(up - B, 0)] == m)
            Kq[gi, :, nn] = cols; par[gi, m] = nn
            fo[gi[hit], up[hit] - B] = nn[hit]; fo[gi, nn - B] = m
            Xq[gi, :, nn] = (xs[gi, :, li] + zz[gi, :, li]) >> 1
            A[r] = int(np.sum(live & ~seat))
            z[r] = (zz + xs) >> 1; b[r] = s
        if t > 0:
            for q in range(N):
                r = (q - t) % N; o = b0[r]; gi, li = np.nonzero(lowest(o))
                TR[(q - 1) % N][gi, o[gi, li]] = b[r][gi, li]
        b0 = b.copy()
        if t < VIS - 1:
            for q in range(N):
                r = (q - t) % N; b[r] = np.take_along_axis(TR[q], b0[r], 1)
    zq = np.stack([z[(q - VIS + 1) % N] for q in range(N)])
    return {"yk": np.ascontiguousarray(KN[:, :, :, B:]).reshape(N, 128, J).astype(np.float32), "yp": np.ascontiguousarray(KN[:, :, 0, :B]).astype(np.float32), "yf": FT.astype(np.float32),
            "yt": TR.astype(np.float32), "yx": np.ascontiguousarray(X[:, :, :, B:]).reshape(N, 128, J).astype(np.float32).astype(BF), "yz": zq.reshape(N, 128, L).astype(np.float32).astype(BF)}

@@ -1,0 +1,458 @@
+from concourse.mybir import AluOpType as A, AxisListType, ActivationFunctionType as AF
+
+NW, NB, NJ, VIS, ST = 3584, 2560, 1024, 4, 3
+WN = 3856
+DA, DB = 3600, 3728
+WT = 2176.0
+M7, M0C = 1.5 * 2.0 ** 30, 1.5 * 2.0 ** 23
+CH = [(0, 64), (64, 96), (96, 128)]
+BUFS = {
+    "float32": "KN:3856 FX:3856 TT:3856 OT:3856 ID:3584 TRF:224 ML:48 MS:48 COLF:16 CF:128 C15F:128 CGF:128 D:128 B0:128 R:8 IF:128 GI:136 "
+               "PFF:136 R0:272 RS:256 I8:8 J8:8 DUM:40 NN:64 BO:96 BSS:128 NR:1024 VF:1024 FVO:256 CFR:128 FP:16 VM:272 RR:16 FF:16 T1:8 "
+               "E:128 HO:128 EM:128 TM:128 TS:128 TB1:8 MU:256 MS1:256 GO:128 GZ:128 UM:128 MU2:256 MS2:256 SQ:16 SQ2:16 NLV:16 CE:16 "
+               "CO:24 OF:32 BLF:8 ZS:128 ZQ:128 VK:256 MAY:8 CND:32 AS:4 OR:128",
+    "bfloat16": "X:3856 XW:3584 BT:4096 Z0:128 ZL:384 ZN:512 ZR:2048 RB:8 IB:128 ONB:128 WB:16 NU:128 PB:272 CK:272 RSB:256 BCB:512 DIFF:2048 "
+                "AB:2048 DFB:128 ABB:128 CHB:128 CB8:8 CDE:128 CDO:128 ME:128 MH:128 MX:128 ML2:16 EQ:1024 E2:256 H2:256 EM2:256 LA:8",
+    "int32": "KI:3584 FI:1024 BI:128 TRI:224 CI:128 C15:128 CG:128 COLI:4 NI:32 BC:384 AI:4",
+    "uint16": "CL:64 BL:320 KL:128 YL:16 LO:24 VL:8 LS:32 L8:8",
+}
+SCRATCH = {"TD": ("dram", [128, 224], "float32"), "TB": ("dram", [128, 224], "float32"), "TBL": ("dram", [128, 224], "float32"),
+           "BTD": ("dram", [16, 128, 32], "bfloat16")}
+for _d in BUFS:
+    for _b in BUFS[_d].split():
+        SCRATCH[_b.split(":")[0]] = ("sbuf", [128, int(_b.split(":")[1])], _d)
+for _i in range(8):
+    SCRATCH["ps%d" % _i] = ("psum", [128, 512], "float32")
+SEMAPHORES = ["V", "S", "P", "G", "kn0", "kn1", "kn2", "kn3", "lx", "lw", "lf", "lb", "lz", "lt", "btd", "bt", "tt", "tb", "ot", "out",
+              "aT", "aB", "aTB", "loc"] + ["a%s%d" % (k, t) for k in "CZM" for t in range(3)]
+
+
+def rank_program(g, core, T, topo):
+    rank = T.rank_of(core)
+    if rank is None:
+        return
+    cores = T.cores
+    n = len(cores)
+    Q = {"V": g.vector, "S": g.scalar, "P": g.tensor, "G": g, "Y": g.sync}
+    tot, waited, last, readers, excl = {}, {}, {}, {}, {}
+
+    def need(eng, sem, val):
+        val = tot[sem] if val is None else val
+        if waited.get((eng, sem), 0) < val:
+            Q[eng].wait_ge(T.sem[sem], val)
+            waited[(eng, sem)] = val
+
+    def before(eng, rd, wr, ps):
+        for k in rd:
+            if k in last:
+                need(eng, last[k][0], last[k][1])
+        for k in wr:
+            if k in last:
+                need(eng, last[k][0], last[k][1])
+            for s, v in readers.get(k, {}).items():
+                if s != eng:
+                    need(eng, s, v)
+        for k in ps:
+            for s, v in excl.get(k, {}).items():
+                if s != eng:
+                    need(eng, s, v)
+
+    def after(sem, val, rd, wr, ps):
+        for k in rd:
+            readers.setdefault(k, {})[sem] = val
+        for k in wr:
+            last[k] = (sem, val)
+            readers[k] = {}
+        for k in ps:
+            excl.setdefault(k, {})[sem] = val
+
+    def op(eng, fn, rd, wr, ps):
+        rd, wr, ps = rd.split(), wr.split(), ps.split()
+        before(eng, rd, wr, ps)
+        fn().then_inc(T.sem[eng], 1)
+        tot[eng] = tot.get(eng, 0) + 1
+        after(eng, tot[eng], rd, wr, ps)
+
+    def ts(out, in0, s1, op0, s2=None, op1=None, rd="", wr="", ps=""):
+        if op1 is None:
+            op("V", lambda: g.vector.tensor_scalar(out=out, in0=in0, scalar1=s1, scalar2=None, op0=op0), rd, wr, ps)
+        else:
+            op("V", lambda: g.vector.tensor_scalar(out=out, in0=in0, scalar1=s1, scalar2=s2, op0=op0, op1=op1), rd, wr, ps)
+
+    def tt(out, in0, in1, o, rd="", wr="", ps=""):
+        op("V", lambda: g.vector.tensor_tensor(out=out, in0=in0, in1=in1, op=o), rd, wr, ps)
+
+    def cp(out, in_, rd="", wr="", ps=""):
+        op("V", lambda: g.vector.tensor_copy(out=out, in_=in_), rd, wr, ps)
+
+    def scan(out, d0, d1, init, o0, o1, rd="", wr="", ps=""):
+        op("V", lambda: g.vector.tensor_tensor_scan(out=out, data0=d0, data1=d1, initial=init, op0=o0, op1=o1), rd, wr, ps)
+
+    def fill(ap, c, wr):
+        op("V", lambda: g.vector.memset(ap, c), "", wr, "")
+
+    def act(out, in_, f, rd="", wr="", ps="", **kw):
+        op("S", lambda: g.scalar.activation(out=out, in_=in_, func=f, **kw), rd, wr, ps)
+
+    def mm(out, l, r, a, z, rd="", ps=""):
+        op("P", lambda: g.tensor.matmul(out=out, lhsT=l, rhs=r, start=a, stop=z), rd, "", ps)
+
+    def iota(out, pat, base, cm, wr, flag=True):
+        if flag:
+            op("G", lambda: g.iota(out=out, pattern=pat, base=base, channel_multiplier=cm, allow_small_or_imprecise_dtypes=True), "", wr, "")
+        else:
+            op("G", lambda: g.iota(out=out, pattern=pat, base=base, channel_multiplier=cm), "", wr, "")
+
+    def dma(eng, grp, out, in_, rd="", wr=""):
+        rd, wr = rd.split(), wr.split()
+        for k in rd:
+            if k in last:
+                need(eng, last[k][0], last[k][1])
+        for k in wr:
+            if k in last and last[k][0] != grp:
+                need(eng, last[k][0], last[k][1])
+            for s, v in readers.get(k, {}).items():
+                need(eng, s, v)
+        Q[eng].dma_start(out=out, in_=in_).then_inc(T.sem[grp], 16)
+        tot[grp] = tot.get(grp, 0) + 16
+        after(grp, None, rd, wr, [])
+
+    def send(dst, out, in_, sem, rd):
+        before("G", rd.split(), [], [])
+        rid, pid, _ = topo.addr(dst)
+        m = 0
+        for e in topo.engines(core, dst)[:8]:
+            m |= 1 << e
+        g.remote_dma(out, in_, T.sem[sem], T.sem.loc, pid, rid, m)
+        tot["loc"] = tot.get("loc", 0) + 8
+
+    def arrives(sem, key):
+        tot[sem] = 8
+        last[key] = (sem, 8)
+        readers[key] = {}
+
+    nxt, prv = cores[(rank + 1) % n], cores[(rank - 1) % n]
+    lo = [NB + 128 * ((rank - t) % n) for t in range(VIS)]
+    D, RS, DP = T.D[:], T.RS, T.ps7
+    PF, P15, PG, PP, OD, EV, M0, NM0, WA0 = [T.COLF[:, i:i + 1] for i in range(9)]
+    PI, P15I, PGI, PEI = [T.COLI[:, i:i + 1] for i in range(4)]
+
+    for i in range(4):
+        dma("Y", "kn%d" % i, T.KI[:, 896 * i:896 * i + 896], T.kn[:, 896 * i:896 * i + 896], wr="KI%d" % i)
+    for p in range(16):
+        dma("S", "lf", T.FI[p::16, :], T.ft[:], wr="FI")
+    dma("S", "lt", T.TRI[:], T.tr[:], wr="TRI")
+    dma("Y", "lx", T.X[:, 0:NW], T.x0[:], wr="XL")
+    for p in range(16):
+        dma("S", "lb", T.BI[p::16, :], T.bs[:], wr="BI")
+    dma("S", "lz", T.Z0[:], T.z0[:], wr="Z0")
+    dma("Y", "lw", T.XW[:], T.x0[:], wr="XW")
+
+    iota(T.CI[:], [[1, 128]], 0, 0, "CI", False)
+    iota(PI, [[0, 1]], 0, 1, "PI", False)
+    iota(T.CF[:], [[1, 128]], 0, 0, "CF")
+    iota(PF, [[0, 1]], 0, 1, "PF")
+    iota(T.I8[:], [[16, 8]], 0, 0, "I8")
+    iota(T.GI[:], [[17, 8], [1, 17]], 0, 0, "GI")
+    iota(T.NI[:], [[1, 32]], 0, 32, "NI", False)
+    ts(P15I, PI, 15, A.bitwise_and, rd="PI", wr="P15I")
+    ts(PGI, PI, 4, A.arith_shift_right, rd="PI", wr="PGI")
+    ts(T.C15[:], T.CI[:], 15, A.bitwise_and, rd="CI", wr="C15")
+    ts(T.CG[:], T.CI[:], 4, A.arith_shift_right, rd="CI", wr="CG")
+    ts(PEI, PI, 4, A.arith_shift_right, 1, A.bitwise_and, rd="PI", wr="PEI")
+    cp(P15, P15I, "P15I", "P15")
+    cp(PG, PGI, "PGI", "PG")
+    cp(T.C15F[:], T.C15[:], "C15", "C15F")
+    cp(T.CGF[:], T.CG[:], "CG", "CGF")
+    cp(OD, PEI, "PEI", "OD")
+    ts(T.D[:], T.C15F[:], P15, A.is_equal, rd="C15F P15", wr="D")
+    ts(M0, P15, 0.0, A.is_equal, rd="P15", wr="M0")
+    ts(NM0, P15, 0.0, A.not_equal, rd="P15", wr="NM0")
+    ts(T.B0[:], T.CGF[:], PG, A.is_equal, M0, A.mult, rd="CGF PG M0", wr="B0")
+    cp(DP[:, 0:128], D, "D", "DP")
+    cp(DP[:, 128:256], D, "D", "DP")
+    fill(T.RS[:], 1.0, "RS")
+    fill(T.RS[:, 0::16], 0.0, "RS")
+    ts(T.J8[:], T.I8[:], P15, A.add, rd="I8 P15", wr="J8")
+    for i, d in enumerate((DA, DA, DB, DA, DA)):
+        ts(T.DUM[:, 8 * i:8 * i + 8], T.J8[:], float(d), A.add, rd="J8", wr="DUM")
+    for t in range(VIS):
+        ts(T.NN[:, 16 * t:16 * t + 8], T.J8[:], float(lo[t]), A.add, rd="J8", wr="NN")
+        ts(T.NN[:, 16 * t + 8:16 * t + 16], T.J8[:], float(lo[t]), A.add, rd="J8", wr="NN")
+        fill(T.BO[:, 24 * t + 16:24 * t + 24], float(lo[t] - DB), "BO")
+        fill(T.BSS[:, 32 * t + 8:32 * t + 16], float(lo[t] - DB), "BSS")
+    fill(T.FX[:, 0:NB], -1.0, "FX")
+    fill(T.FX[:, NW:WN], -1.0, "FX")
+    fill(T.KN[:, NW:WN], -1.0, "KN")
+    cp(T.FX[:, NB:NW], T.FI[:], "FI", "FX")
+    cp(T.TRF[:], T.TRI[:], "TRI", "TRF")
+    for i in range(4):
+        cp(T.KN[:, 896 * i:896 * i + 896], T.KI[:, 896 * i:896 * i + 896], "KI%d" % i, "KN")
+    send(nxt, T.TD[:], T.TRF[:], "aT", "TRF")
+    arrives("aT", "TD")
+
+    def constants2():
+        ts(T.IF[:], T.CF[:], PF, A.is_equal, rd="CF PF", wr="IF")
+        ts(T.R[:], T.CGF[:, 0::16], PG, A.is_equal, rd="CGF PG", wr="R")
+        cp(T.RB[:], T.R[:], "R", "RB")
+        ts(T.WB[:, 0:8], T.R[:], WT, A.mult, rd="R", wr="WB")
+        ts(T.WB[:, 8:16], T.R[:], WT, A.mult, rd="R", wr="WB")
+        fill(T.ONB[:], 1.0, "ONB")
+        tt(PP, PF, PG, A.add, "PF PG", "PP0")
+        ts(PP, PP, 1.0, A.add, rd="PP0", wr="PP")
+        ts(T.PB[:, 0:136], T.GI[:], PP, A.is_equal, 1.0 / 64, A.mult, rd="GI PP", wr="PB")
+        ts(T.PB[:, 136:272], T.GI[:], PP, A.is_equal, -1.0, A.mult, rd="GI PP", wr="PB")
+        ts(T.PFF[:], T.GI[:], PP, A.is_equal, rd="GI PP", wr="PFF")
+        fill(T.CK[:], 0.0, "CK")
+        iota(T.CK[0:1, :], [[0, 16], [128, 17]], 0, 0, "CK")
+        fill(T.CK[32:33, 0:136], -161.0, "CK")
+        fill(T.CK[32:33, 136:272], 8192.0, "CK")
+        fill(T.CK[64:65, 136:272], 32.0, "CK")
+        fill(T.CK[32:33, 0::17], 0.0, "CK")
+        fill(T.CK[64:65, 0::17], 0.0, "CK")
+        fill(T.R0[:], -1.0e9, "R0")
+        fill(T.R0[:, 0::17], 1.0e9, "R0")
+        fill(T.E[:], 0.0, "E")
+        fill(WA0, 0.0, "WA0")
+
+    def constants3():
+        iota(T.ID[:], [[1, NW]], 0, 0, "ID")
+        ts(T.IB[:], T.CF[:], PF, A.is_equal, rd="CF PF", wr="IB")
+        ts(EV, OD, 0.0, A.is_equal, rd="OD", wr="EV")
+        ts(T.NU[:], T.CF[:], PF, A.is_le, -32.0, A.mult, rd="CF PF", wr="NU")
+        fill(T.RSB[:], 1.0, "RSB")
+        fill(T.RSB[:, 0::16], 0.0, "RSB")
+        fill(T.ME[:], 0.0, "ME")
+        fill(T.E2[:], 0.0, "E2")
+        fill(T.ML2[:], 1.0, "ML2")
+        fill(T.NR[:], 0.0, "NR")
+        fill(T.MS[:], 0.0, "MS")
+        fill(T.X[:, NW:WN], 0.0, "XL")
+        fill(T.TT[:, NW:WN], 0.0, "TT")
+        for t in range(VIS):
+            ts(T.NR[:, 256 * t:256 * t + 128], T.CF[:], float(lo[t]), A.add, M0, A.mult, rd="CF M0", wr="NR")
+            ts(T.VF[:, 256 * t + 128:256 * t + 256], T.CF[:], float(lo[t]), A.add, rd="CF", wr="VFr")
+        fill(T.BCB[:, 384:512], 0.0, "BCB")
+        for b in range(12):
+            ts(T.BC[:, 32 * b:32 * b + 32], T.NI[:], b, A.arith_shift_right, 1, A.bitwise_and, rd="NI", wr="BC")
+        ts(T.BCB[:, 0:384], T.BC[:], 2.0, A.mult, -1.0, A.add, rd="BC", wr="BCB")
+        for b in range(16):
+            dma("Y", "btd", T.BTD[b], T.BCB[:, 32 * b:32 * b + 32], rd="BCB", wr="BTD")
+        for i in range(8):
+            dma("Y", "bt", T.BT[16 * i:16 * i + 16, :], T.BTD[:], rd="BTD", wr="BT")
+        for p in range(16):
+            dma("Y", "tt", T.TT[p::16, 0:NW], T.TD[:], rd="TD", wr="TTd")
+
+    def kwin():
+        return T.KN[:, 0:WN]
+
+    def out(t):
+        a, z = lo[t], lo[t] + 128
+        mm(T.ps2[:, 0:128], T.B0[:], T.KN[:, a:z], True, True, "B0 KN", "ps2")
+        tt(T.MU[:, 0:128], T.FX[:, a:z], DP[:, 0:128], A.mult, "FX DP", "MUa")
+        act(T.FVO[:, 0:128], T.FX[:, a:z], AF.Copy, "FX", "FVO")
+        act(T.UM[:], T.KN[:, a:z], AF.Copy, "KN M0", "UM", scale=M0)
+        tt(T.MU[:, 128:256], T.ps2[:, 0:128], D, A.mult, "D", "MUb", "ps2")
+        scan(T.MS1[:], RS[:], T.MU[:], 0.0, A.mult, A.add, "RS MUa MUb", "MS1")
+        cp(T.YL[:], T.MS1[:, 15::16], "MS1", "YL")
+        act(T.GO[:], kwin().indirect(T.YL[:, 0:8]), AF.Copy, "KN YL", "GO")
+        mm(T.ps2[:, 0:128], T.B0[:], T.GO[:], True, True, "B0 GO", "ps2")
+        act(T.GZ[:], T.GO[:], AF.Copy, "GO NM0", "GZ", scale=NM0)
+        tt(T.MU2[:, 128:256], T.FX[:, 0:WN].indirect(T.YL[:, 8:16]), D, A.mult, "FX YL D", "MU2b")
+        ts(T.SQ[:], T.MS1[:, 15::16], a + 63.5, A.subtract, rd="MS1", wr="SQ")
+        tt(T.BO[:, 24 * t:24 * t + 16], T.MS1[:, 15::16], T.DUM[:, 0:16], A.subtract, "MS1 DUM", "BO")
+        tt(T.SQ2[:], T.SQ[:], T.SQ[:], A.mult, "SQ", "SQ2")
+        ts(T.NLV[:], T.SQ2[:], 4096.0, A.is_ge, rd="SQ2", wr="NLV")
+        tt(T.CO[:, 16:24], T.NLV[:, 0:8], T.NLV[:, 8:16], A.mult, "NLV", "COc")
+        tt(T.MU2[:, 0:128], T.ps2[:, 0:128], D, A.mult, "D", "MU2a", "ps2")
+        scan(T.MS2[:], RS[:], T.MU2[:], 0.0, A.mult, A.add, "RS MU2a MU2b", "MS2")
+        tt(T.CE[:], T.MS2[:, 15::16], T.NN[:, 16 * t:16 * t + 16], A.is_equal, "MS2 NN", "CE")
+        tt(T.CO[:, 0:8], T.CE[:, 0:8], T.CO[:, 16:24], A.mult, "CE COc", "COa")
+        tt(T.CO[:, 8:16], T.CE[:, 8:16], T.CO[:, 0:8], A.mult, "CE COa", "COb")
+        tt(T.OF[:, 0:24], T.CO[:], T.BO[:, 24 * t:24 * t + 24], A.mult, "COa COb COc BO", "OF")
+        tt(T.OF[:, 0:24], T.OF[:, 0:24], T.DUM[:, 0:24], A.add, "OF DUM", "OF")
+        cp(T.LO[:], T.OF[:, 0:24], "OF", "LO")
+        tt(kwin().indirect(T.LO[:, 0:8]), T.GZ[:], T.UM[:], A.add, "LO GZ UM", "KN")
+        cp(T.FX[:, 0:WN].indirect(T.LO[:, 8:24]), T.FVO[:], "LO FVO FVOr", "FX")
+
+    def start(t, rows, rkey):
+        tt(T.TM[:], rows, D, A.mult, rkey + " D", "TM")
+        scan(T.TS[:], RS[:, 0:128], T.TM[:], 0.0, A.mult, A.add, "RS TM", "TS")
+        i = 16 * (4 * t)
+        cp(T.BL[:, i:i + 8], T.TS[:, 15::16], "TS", "BL%d" % (4 * t))
+        mm(T.ps6[:, 0:8], T.TM[:], T.R[:], True, True, "TM R", "ps6")
+
+    def zrep(zz, key):
+        for k in range(16):
+            if k < 10:
+                cp(T.ZR[:, k::16], zz, key, "ZRv")
+            else:
+                act(T.ZR[:, k::16], zz, AF.Copy, key, "ZRs")
+
+    def step(t, s, zz, zkey, wa, wkey):
+        q = 4 * t + s
+        bl, bk = T.BL[:, 16 * q:16 * q + 8], "BL%d" % q
+        vb, vk = (T.ps0, "ps0") if q % 2 == 0 else (T.ps1, "ps1")
+        mm(vb[:, 0:272], T.ONB[:], T.CK[:], True, False, "ONB CK", vk)
+        cp(T.KL[:], kwin().indirect(bl), "KN " + bk, "KL")
+        act(T.CFR[:], kwin().indirect(bl), AF.Copy, "KN " + bk, "CFR")
+        act(T.CHB[:], T.CFR[:], AF.Identity, "CFR", "CHB", bias=8224.5)
+        mm(vb[:, 136:272], T.CFR[:], T.PFF[:], False, False, "CFR PFF", vk)
+        if s == 0:
+            act(T.CB8[:], T.ps6[:, 0:8], AF.Identity, "", "CB8", "ps6", bias=8224.5)
+            zrep(zz, zkey)
+            tt(T.TB1[:], T.ps6[:, 0:8], T.CB8[:], A.subtract, "CB8", "TB1", "ps6")
+        tt(T.DFB[:], T.X[:, 0:NW].indirect(bl), zz, A.subtract, "X XL " + bk + " " + zkey, "DFB")
+        if s == 0:
+            act(T.FF[:, 0:8], T.CB8[:], AF.Identity, "CB8", "FF", scale=1.0 / 64, bias=-161.0)
+            act(T.FF[:, 8:16], T.TB1[:], AF.Identity, "TB1", "FF", bias=8224.0)
+        act(T.ABB[:], T.DFB[:], AF.Abs, "DFB", "ABB")
+        mm(vb[:, 0:272:17], T.ABB[:], T.WB[:], False, False, "ABB WB", vk)
+        for c, (a, z) in enumerate(CH):
+            tt(T.DIFF[:, 16 * a:16 * z], T.XW[:].indirect(T.KL[:, a:z]), T.ZR[:, 16 * a:16 * z], A.subtract, "XW KL ZRv ZRs", "DF%d" % c)
+            act(T.AB[:, 16 * a:16 * z], T.DIFF[:, 16 * a:16 * z], AF.Abs, "DF%d" % c, "AB%d" % c)
+            for k in range(16):
+                mm(vb[a:z, k + 1:272:17], T.AB[:, 16 * a + k:16 * z:16], T.WB[:], False, False, "AB%d WB" % c, vk)
+            if c == 1:
+                act(T.FP[:], T.FF[:], AF.Identity, "FF " + wkey, "FP", bias=wa)
+                mm(vb[:, 0:272:17], T.IF[:], T.FP[:], False, False, "IF FP", vk)
+        mm(vb[:, 0:272], T.CHB[:], T.PB[:], False, True, "CHB PB", vk)
+        scan(T.VM[:], T.R0[:], vb[:, 0:272], 1.0e9, A.max, A.min, "R0", "VM", vk)
+        ts(T.RR[:], T.VM[:, 16::17], M7, A.add, M7, A.subtract, rd="VM", wr="RR")
+        tt(T.FF[:], T.VM[:, 16::17], T.RR[:], A.subtract, "VM RR", "FF")
+        ts(T.T1[:], T.FF[:, 0:8], 64.0, A.mult, 2080.0, A.add, rd="FF", wr="T1")
+        tt(T.E[:, 0::16], T.T1[:], T.FF[:, 8:16], A.add, "T1 FF", "E")
+        scan(T.HO[:], RS[:, 0:128], T.E[:], 0.0, A.mult, A.add, "RS E", "HO")
+        tt(T.EM[:], T.HO[:], DP[:, 0:128], A.mult, "HO DP", "EM")
+        mm(T.ps6[:, 0:8], T.EM[:], T.R[:], True, True, "EM R", "ps6")
+        cp(T.BL[:, 16 * q + 16:16 * q + 24], T.ps6[:, 0:8], "", "BL%d" % (q + 1), "ps6")
+
+    def seat(t, zz, zkey):
+        fin = t == VIS - 1
+        a = lo[t]
+        q = 4 * t + 3
+        bl, bk = T.BL[:, 16 * q:16 * q + 8], "BL%d" % q
+        zn, znk = T.ZN[:, 128 * t:128 * t + 128], "ZN%d" % t
+        vf = T.VF[:, 256 * t:256 * t + 256]
+        if fin:
+            send(prv, T.CL[:, 48:56], bl, "aB", bk)
+        else:
+            send(nxt, T.CL[:, 16 * t:16 * t + 8], bl, "aC%d" % t, bk)
+        act(T.VK[:, 128:256], kwin().indirect(bl), AF.Copy, "KN " + bk, "VKb")
+        mm(T.ps2[:, 0:128], T.B0[:], T.VK[:, 128:256], True, True, "B0 VKb", "ps2")
+        act(T.CDE[:], T.BT[:].indirect(bl), AF.Copy, "BT EV " + bk, "CDE", scale=EV)
+        act(T.CDO[:], T.BT[:].indirect(bl), AF.Copy, "BT OD " + bk, "CDO", scale=OD)
+        for h in range(2):
+            ps, pk = (T.ps3, "ps3") if h == 0 else (T.ps4, "ps4")
+            for i in range(4):
+                gr = 4 * h + i
+                r = 32 * (gr // 2)
+                cd, ck = (T.CDE, "CDE") if gr % 2 == 0 else (T.CDO, "CDO")
+                mm(ps[:, 128 * i:128 * i + 128], T.IB[:], T.NU[:], True, False, "IB NU", pk)
+                if i == 2:
+                    need("P", "P", tot["P"])
+                mm(ps[:, 128 * i:128 * i + 128], cd[r:r + 32, :], cd[r:r + 32, :], False, True, ck, pk)
+            act(T.EQ[:, 512 * h:512 * h + 512], ps[:], AF.Relu, "", "EQ%d" % h, pk, bias=-11.0)
+        tt(T.ZS[:], T.X[:, 0:NW].indirect(bl), zz, A.add, "X XL " + bk + " " + zkey, "ZS")
+        ts(T.ZQ[:], T.ZS[:], 0.4999, A.mult, M0C, A.add, rd="ZS", wr="ZQ")
+        ts(zn, T.ZQ[:], -M0C, A.add, rd="ZQ", wr=znk)
+        if not fin:
+            send(nxt, T.ZL[:, 128 * t:128 * t + 128], zn, "aZ%d" % t, znk)
+        cp(T.BLF[:], T.ps6[:, 0:8], "", "BLF", "ps6")
+        ts(T.SQ[:, 0:8], T.BLF[:], a + 63.5, A.subtract, rd="BLF", wr="SQ")
+        tt(T.MU[:, 0:128], T.ps2[:, 0:128], D, A.mult, "D", "MUa", "ps2")
+        tt(T.SQ2[:, 0:8], T.SQ[:, 0:8], T.SQ[:, 0:8], A.mult, "SQ", "SQ2")
+        scan(T.MS1[:, 0:128], RS[:, 0:128], T.MU[:, 0:128], 0.0, A.mult, A.add, "RS MUa", "MS1")
+        ts(T.NLV[:, 0:8], T.SQ2[:, 0:8], 4096.0, A.is_ge, rd="SQ2", wr="NLV")
+        cp(T.VL[:], T.MS1[:, 15:128:16], "MS1", "VL")
+        tt(T.ME[:, 0::16], T.NLV[:, 0:8], T.CO[:, 16:24], A.mult, "NLV COc", "ME")
+        tt(T.MAY[:], T.NLV[:, 0:8], T.CO[:, 16:24], A.mult, "NLV COc", "MAY")
+        scan(T.MH[:], T.RSB[:, 0:128], T.ME[:], 0.0, A.mult, A.add, "RSB ME", "MH")
+        tt(T.MU2[:, 0:128], T.FX[:, 0:WN].indirect(T.VL[:]), D, A.mult, "FX VL D", "MU2a")
+        tt(T.MX[:], T.MH[:], DP[:, 0:128], A.mult, "MH DP", "MX")
+        mm(T.ps5[:, 0:8], T.MX[:], T.RB[:], True, True, "MX RB", "ps5")
+        scan(T.MS2[:, 0:128], RS[:, 0:128], T.MU2[:, 0:128], 0.0, A.mult, A.add, "RS MU2a", "MS2")
+        cp(T.ML2[:, 0:8], T.ps5[:, 0:8], "", "ML2", "ps5")
+        act(vf[:, 0:128], T.ID[:].indirect(bl), AF.Copy, "ID " + bk, "VF%d" % t)
+        act(T.VK[:, 0:128], T.VK[:, 128:256], AF.Copy, "VKb NM0", "VKa", scale=NM0)
+        for gr in range(8):
+            mm(T.ps5[:, 16 + gr:32:8], T.EQ[:, 128 * gr:128 * gr + 128], T.ML2[:, gr::8], True, True, "EQ%d ML2" % (gr // 4), "ps5")
+        tt(T.CE[:, 0:8], T.MS2[:, 15:128:16], T.BLF[:], A.is_equal, "MS2 BLF", "CE")
+        b0 = 32 * t
+        tt(T.BSS[:, b0:b0 + 8], T.BLF[:], T.DUM[:, 0:8], A.subtract, "BLF DUM", "BSS")
+        tt(T.BSS[:, b0 + 16:b0 + 24], T.MS1[:, 15:128:16], T.DUM[:, 0:8], A.subtract, "MS1 DUM", "BSS")
+        tt(T.BSS[:, b0 + 24:b0 + 32], T.BLF[:], T.DUM[:, 0:8], A.subtract, "BLF DUM", "BSS")
+        if t in (1, 2):
+            cp(T.L8[:], T.ML[:, 16 * (t - 1):16 * (t - 1) + 8], "M%d" % (t - 1), "L8")
+            cp(T.TT[:].indirect(T.L8[:]), vf[:, 0:128], "L8 VF%d" % t, "TT TTd")
+        ts(T.E2[:, 0::16], T.ps5[:, 16:32], 0.0, A.is_equal, rd="", wr="E2", ps="ps5")
+        scan(T.H2[:], T.RSB[:], T.E2[:], 0.0, A.mult, A.add, "RSB E2", "H2")
+        tt(T.EM2[:], T.H2[:], DP[:, 0:256], A.mult, "H2 DP", "EM2")
+        mm(T.ps5[:, 32:40], T.EM2[:, 0:128], T.RB[:], True, True, "EM2 RB", "ps5")
+        mm(T.ps5[:, 40:48], T.EM2[:, 128:256], T.RB[:], True, True, "EM2 RB", "ps5")
+        tt(T.CND[:, 0:8], T.ps5[:, 32:40], T.MAY[:], A.mult, "MAY", "CN0", "ps5")
+        tt(T.CND[:, 8:16], T.ps5[:, 32:40], T.MAY[:], A.mult, "MAY", "CN1", "ps5")
+        cp(T.CND[:, 24:32], T.ps5[:, 40:48], "", "CN3", "ps5")
+        tt(T.CND[:, 16:24], T.CE[:, 0:8], T.CND[:, 0:8], A.mult, "CE CN0", "CN2")
+        if not fin:
+            tt(T.LA[:], T.CO[:, 16:24], T.CND[:, 0:8], A.subtract, "COc CN0", "LA")
+            mm(T.ps5[:, 48:56], T.ONB[:], T.LA[:], True, True, "ONB LA", "ps5")
+        tt(T.OF[:], T.CND[:], T.BSS[:, b0:b0 + 32], A.mult, "CN0 CN1 CN2 CN3 BSS", "OF")
+        tt(T.OF[:], T.OF[:], T.DUM[:, 8:40], A.add, "OF DUM", "OF")
+        cp(T.LS[:], T.OF[:], "OF", "LS")
+        if not fin:
+            m0 = 16 * t
+            cp(T.MS[:, m0:m0 + 8], T.OF[:, 24:32], "OF", "MS")
+            op("V", lambda: g.vector.tensor_reduce(out=T.AS[:, 0:1], in_=T.ps5[:, 48:56], axis=AxisListType.X, op=A.add), "", "AS", "ps5")
+            cp(T.AI[:, 0:1], T.AS[:, 0:1], "AS", "AI0")
+            ts(T.AI[:, 1:2], T.AI[:, 0:1], 31, A.bitwise_and, rd="AI0", wr="AI1")
+            ts(T.MS[:, m0 + 8:m0 + 9], T.AI[:, 1:2], WT, A.mult, rd="AI1", wr="MS")
+            send(nxt, T.ML[:, m0:m0 + 16], T.MS[:, m0:m0 + 16], "aM%d" % t, "MS")
+            if t == 2:
+                cp(T.L8[:], T.OF[:, 24:32], "OF", "L8")
+        tt(kwin().indirect(T.LS[:, 0:16]), T.VK[:], T.NR[:, 256 * t:256 * t + 256], A.add, "LS VKa VKb NR", "KN")
+        cp(T.FX[:, 0:WN].indirect(T.LS[:, 8:24]), vf, "LS VF%d VFr" % t, "FX")
+        cp(T.X[:].indirect(T.LS[:, 8:16]), zn, "LS " + znk, "X XL")
+        if not fin:
+            act(T.XW[:, a:a + 128], T.X[:, a:a + 128], AF.Copy, "X", "XW")
+
+    fill(T.FVO[:, 128:256], float(NW), "FVOr")
+    constants2()
+    out(0)
+    start(0, T.BI[:], "BI")
+    fill(T.XW[:, lo[0]:lo[0] + 128], 4096.0, "XW")
+    for t in range(VIS):
+        if t == 0:
+            zz, zkey, wa, wkey = T.Z0[:], "Z0", WA0, "WA0"
+        else:
+            u = t - 1
+            arrives("aC%d" % u, "CL%d" % u)
+            arrives("aZ%d" % u, "ZL%d" % u)
+            arrives("aM%d" % u, "M%d" % u)
+            zz, zkey = T.ZL[:, 128 * u:128 * u + 128], "ZL%d" % u
+            wa, wkey = T.ML[:, 16 * u + 8:16 * u + 9], "M%d" % u
+            start(t, T.TT[:].indirect(T.CL[:, 16 * u:16 * u + 8]), "TT TTd CL%d" % u)
+        for s in range(ST):
+            step(t, s, zz, zkey, wa, wkey)
+            if t == 0 and s == 0:
+                constants3()
+        seat(t, zz, zkey)
+        if t == 2:
+            dma("Y", "tb", T.TB[:], T.TT[0::16, 0:NW], rd="TT", wr="TB")
+            send(prv, T.TBL[:], T.TB[:], "aTB", "TB")
+            arrives("aTB", "TBL")
+            dma("Y", "ot", T.OT[0::16, 0:NW], T.TBL[:], rd="TBL", wr="OT")
+        if t < VIS - 1:
+            fill(T.XW[:, lo[t + 1]:lo[t + 1] + 128], 4096.0, "XW")
+            out(t + 1)
+    arrives("aB", "CLB")
+    act(T.OR[:], T.ID[:].indirect(T.CL[:, 48:56]), AF.Copy, "ID CLB", "OR")
+    dma("Y", "out", T.yz[:], T.ZN[:, 384:512], rd="ZN3")
+    dma("S", "out", T.yk[:], T.KN[:, NB:NW], rd="KN")
+    dma("Y", "out", T.yp[:], T.KN[0::16, 0:NB], rd="KN")
+    dma("S", "out", T.yf[:], T.FX[0::16, NB:NW], rd="FX")
+    dma("Y", "out", T.yx[:], T.X[:, NB:NW], rd="X")
+    cp(T.OT[:].indirect(T.L8[:]), T.OR[:], "L8 OR", "OT")
+    dma("Y", "out", T.yt[:], T.OT[0::16, 0:NW], rd="OT")
+    for s in list(tot):
+        need("G", s, tot[s])

@@ -1,23 +1,25 @@
-from concourse.mybir import AluOpType as A, AxisListType, ActivationFunctionType as AF
+from concourse.mybir import AluOpType as A, ActivationFunctionType as AF
 
 NW, NB, NJ, VIS, ST = 3584, 2560, 1024, 4, 3
 WN = 3856
 DA, DB = 3600, 3728
 WT = 2176.0
 M7, M0C = 1.5 * 2.0 ** 30, 1.5 * 2.0 ** 23
-CH = [(0, 64), (64, 96), (96, 128)]
+CH = [(0, 64), (64, 96), (96, 112), (112, 128)]
+PE = {0: (0, 64), 1: (64, 96), 3: (96, 128)}
 BUFS = {
     "float32": "KN:3856 FX:3856 TT:3856 OT:3856 ID:3584 TRF:224 ML:48 MS:48 COLF:16 CF:128 C15F:128 CGF:128 D:128 B0:128 R:8 IF:128 GI:136 "
-               "PFF:136 R0:272 RS:256 I8:8 J8:8 DUM:40 NN:64 BO:96 BSS:128 NR:1024 VF:1024 FVO:256 CFR:128 FP:16 VM:272 RR:16 FF:16 T1:8 "
-               "E:128 HO:128 EM:128 TM:128 TS:128 TB1:8 MU:256 MS1:256 GO:128 GZ:128 UM:128 MU2:256 MS2:256 SQ:16 SQ2:16 NLV:16 CE:16 "
-               "CO:24 OF:32 BLF:8 ZS:128 ZQ:128 VK:256 MAY:8 CND:32 AS:4 OR:128",
-    "bfloat16": "X:3856 XW:3584 BT:4096 Z0:128 ZL:384 ZN:512 ZR:2048 RB:8 IB:128 ONB:128 WB:16 NU:128 PB:272 CK:272 RSB:256 BCB:512 DIFF:2048 "
-                "AB:2048 DFB:128 ABB:128 CHB:128 CB8:8 CDE:128 CDO:128 ME:128 MH:128 MX:128 ML2:16 EQ:1024 E2:256 H2:256 EM2:256 LA:8",
-    "int32": "KI:3584 FI:1024 BI:128 TRI:224 CI:128 C15:128 CG:128 COLI:4 NI:32 BC:384 AI:4",
+               "PFF:136 R0:272 RS:256 I8:8 J8:8 DUM:40 NN:64 BO:96 BSS:128 NR:1024 VF:1024 FVO:256 CFR:128 FP:16 VM:272 RR:16 FF:16 "
+               "TM:128 TS:128 TB1:8 MU:256 MS1:256 GO:128 GZ:128 UM:128 MU2:256 MS2:256 SQ2:16 NLV:16 CE:16 "
+               "CO:24 OF:32 BLF:8 ZS:128 ZQ:128 VK:256 CND:32 AQ:8 WAQ:4 OR:128",
+    "bfloat16": "X:3856 XW:3584 BT:4096 Z0:128 ZL:384 ZN:512 ZR:2048 RB:8 RB64:8 E:256 HO:256 EM:256 IB:128 ONB:128 WB:16 NU:128 PB:272 "
+                "CK:272 RSB:256 BCB:1024 DIFF:2048 AB:2048 DFB:128 ABB:128 CHB:128 CB8:8 CDE:128 CDO:128 ME:128 MH:128 MX:128 ML2:16 "
+                "EQ:1024 E2:256 H2:256 EM2:256 LA:8",
+    "int32": "KI:3584 FI:1024 BI:128 TRI:224 CI:128 C15:128 CG:128 COLI:4 NI:64 BC:768 AI:4",
     "uint16": "CL:64 BL:320 KL:128 YL:16 LO:24 VL:8 LS:32 L8:8",
 }
 SCRATCH = {"TD": ("dram", [128, 224], "float32"), "TB": ("dram", [128, 224], "float32"), "TBL": ("dram", [128, 224], "float32"),
-           "BTD": ("dram", [16, 128, 32], "bfloat16")}
+           "BTD": ("dram", [16, 64, 64], "bfloat16")}
 for _d in BUFS:
     for _b in BUFS[_d].split():
         SCRATCH[_b.split(":")[0]] = ("sbuf", [128, int(_b.split(":")[1])], _d)
@@ -137,7 +139,7 @@ def rank_program(g, core, T, topo):
     PF, P15, PG, PP, OD, EV, M0, NM0, WA0 = [T.COLF[:, i:i + 1] for i in range(9)]
     PI, P15I, PGI, PEI = [T.COLI[:, i:i + 1] for i in range(4)]
 
-    for i in range(4):
+    for i in (3, 2, 0, 1):
         dma("Y", "kn%d" % i, T.KI[:, 896 * i:896 * i + 896], T.kn[:, 896 * i:896 * i + 896], wr="KI%d" % i)
     for p in range(16):
         dma("S", "lf", T.FI[p::16, :], T.ft[:], wr="FI")
@@ -148,13 +150,24 @@ def rank_program(g, core, T, topo):
     dma("S", "lz", T.Z0[:], T.z0[:], wr="Z0")
     dma("Y", "lw", T.XW[:], T.x0[:], wr="XW")
 
+    iota(T.NI[0:64, :], [[1, 64]], 0, 64, "NI", False)
+    fill(T.CK[:], 0.0, "CK")
+    iota(T.CK[0:1, :], [[0, 16], [128, 17]], 0, 0, "CK")
     iota(T.CI[:], [[1, 128]], 0, 0, "CI", False)
     iota(PI, [[0, 1]], 0, 1, "PI", False)
     iota(T.CF[:], [[1, 128]], 0, 0, "CF")
     iota(PF, [[0, 1]], 0, 1, "PF")
     iota(T.I8[:], [[16, 8]], 0, 0, "I8")
     iota(T.GI[:], [[17, 8], [1, 17]], 0, 0, "GI")
-    iota(T.NI[:], [[1, 32]], 0, 32, "NI", False)
+    fill(T.BCB[0:64, 768:1024], 0.0, "BCB")
+    for b in range(12):
+        ts(T.BC[0:64, 64 * b:64 * b + 64], T.NI[0:64, :], b, A.arith_shift_right, 1, A.bitwise_and, rd="NI", wr="BC")
+    ts(T.BCB[0:64, 0:768], T.BC[0:64, :], 2.0, A.mult, -1.0, A.add, rd="BC", wr="BCB")
+    for b in range(16):
+        dma("Y", "btd", T.BTD[b], T.BCB[0:64, 64 * b:64 * b + 64], rd="BCB", wr="BTD")
+    for i in range(8):
+        dma("Y", "bt", T.BT[16 * i:16 * i + 16, :], T.BTD[:], rd="BTD", wr="BT")
+    iota(T.FX[:, 0:NB], [[0, NB]], -1, 0, "FXa")
     ts(P15I, PI, 15, A.bitwise_and, rd="PI", wr="P15I")
     ts(PGI, PI, 4, A.arith_shift_right, rd="PI", wr="PGI")
     ts(T.C15[:], T.CI[:], 15, A.bitwise_and, rd="CI", wr="C15")
@@ -181,87 +194,83 @@ def rank_program(g, core, T, topo):
         ts(T.NN[:, 16 * t + 8:16 * t + 16], T.J8[:], float(lo[t]), A.add, rd="J8", wr="NN")
         fill(T.BO[:, 24 * t + 16:24 * t + 24], float(lo[t] - DB), "BO")
         fill(T.BSS[:, 32 * t + 8:32 * t + 16], float(lo[t] - DB), "BSS")
-    fill(T.FX[:, 0:NB], -1.0, "FX")
     fill(T.FX[:, NW:WN], -1.0, "FX")
     fill(T.KN[:, NW:WN], -1.0, "KN")
     cp(T.FX[:, NB:NW], T.FI[:], "FI", "FX")
     cp(T.TRF[:], T.TRI[:], "TRI", "TRF")
-    for i in range(4):
-        cp(T.KN[:, 896 * i:896 * i + 896], T.KI[:, 896 * i:896 * i + 896], "KI%d" % i, "KN")
+    ts(T.IF[:], T.CF[:], PF, A.is_equal, rd="CF PF", wr="IF")
+    ts(T.R[:], T.CGF[:, 0::16], PG, A.is_equal, rd="CGF PG", wr="R")
+    cp(T.RB[:], T.R[:], "R", "RB")
+    ts(T.RB64[:], T.R[:], 64.0, A.mult, rd="R", wr="RB64")
+    fill(T.RSB[:], 1.0, "RSB")
+    fill(T.RSB[:, 0::16], 0.0, "RSB")
+    ts(T.WB[:, 0:8], T.R[:], WT, A.mult, rd="R", wr="WB")
+    ts(T.WB[:, 8:16], T.R[:], WT, A.mult, rd="R", wr="WB")
+    fill(T.ONB[:], 1.0, "ONB")
+    tt(PP, PF, PG, A.add, "PF PG", "PP0")
+    ts(PP, PP, 1.0, A.add, rd="PP0", wr="PP")
+    ts(T.PB[:, 0:136], T.GI[:], PP, A.is_equal, 1.0 / 64, A.mult, rd="GI PP", wr="PB")
+    ts(T.PB[:, 136:272], T.GI[:], PP, A.is_equal, -1.0, A.mult, rd="GI PP", wr="PB")
+    ts(T.PFF[:], T.GI[:], PP, A.is_equal, rd="GI PP", wr="PFF")
+    fill(T.CK[32:33, 0:136], -161.0, "CK")
+    fill(T.CK[32:33, 136:272], 8192.0, "CK")
+    fill(T.CK[64:65, 136:272], 32.0, "CK")
+    fill(T.CK[32:33, 0::17], 0.0, "CK")
+    fill(T.CK[64:65, 0::17], 0.0, "CK")
+    fill(T.R0[:], -1.0e9, "R0")
+    fill(T.R0[:, 0::17], 1.0e9, "R0")
+    fill(T.E[:], 0.0, "E")
+    fill(WA0, 0.0, "WA0")
     send(nxt, T.TD[:], T.TRF[:], "aT", "TRF")
     arrives("aT", "TD")
+    last["XWp"] = last["XW"]
 
-    def constants2():
-        ts(T.IF[:], T.CF[:], PF, A.is_equal, rd="CF PF", wr="IF")
-        ts(T.R[:], T.CGF[:, 0::16], PG, A.is_equal, rd="CGF PG", wr="R")
-        cp(T.RB[:], T.R[:], "R", "RB")
-        ts(T.WB[:, 0:8], T.R[:], WT, A.mult, rd="R", wr="WB")
-        ts(T.WB[:, 8:16], T.R[:], WT, A.mult, rd="R", wr="WB")
-        fill(T.ONB[:], 1.0, "ONB")
-        tt(PP, PF, PG, A.add, "PF PG", "PP0")
-        ts(PP, PP, 1.0, A.add, rd="PP0", wr="PP")
-        ts(T.PB[:, 0:136], T.GI[:], PP, A.is_equal, 1.0 / 64, A.mult, rd="GI PP", wr="PB")
-        ts(T.PB[:, 136:272], T.GI[:], PP, A.is_equal, -1.0, A.mult, rd="GI PP", wr="PB")
-        ts(T.PFF[:], T.GI[:], PP, A.is_equal, rd="GI PP", wr="PFF")
-        fill(T.CK[:], 0.0, "CK")
-        iota(T.CK[0:1, :], [[0, 16], [128, 17]], 0, 0, "CK")
-        fill(T.CK[32:33, 0:136], -161.0, "CK")
-        fill(T.CK[32:33, 136:272], 8192.0, "CK")
-        fill(T.CK[64:65, 136:272], 32.0, "CK")
-        fill(T.CK[32:33, 0::17], 0.0, "CK")
-        fill(T.CK[64:65, 0::17], 0.0, "CK")
-        fill(T.R0[:], -1.0e9, "R0")
-        fill(T.R0[:, 0::17], 1.0e9, "R0")
-        fill(T.E[:], 0.0, "E")
-        fill(WA0, 0.0, "WA0")
-
-    def constants3():
-        iota(T.ID[:], [[1, NW]], 0, 0, "ID")
-        ts(T.IB[:], T.CF[:], PF, A.is_equal, rd="CF PF", wr="IB")
-        ts(EV, OD, 0.0, A.is_equal, rd="OD", wr="EV")
-        ts(T.NU[:], T.CF[:], PF, A.is_le, -32.0, A.mult, rd="CF PF", wr="NU")
-        fill(T.RSB[:], 1.0, "RSB")
-        fill(T.RSB[:, 0::16], 0.0, "RSB")
-        fill(T.ME[:], 0.0, "ME")
-        fill(T.E2[:], 0.0, "E2")
-        fill(T.ML2[:], 1.0, "ML2")
-        fill(T.NR[:], 0.0, "NR")
-        fill(T.MS[:], 0.0, "MS")
-        fill(T.X[:, NW:WN], 0.0, "XL")
-        fill(T.TT[:, NW:WN], 0.0, "TT")
-        for t in range(VIS):
-            ts(T.NR[:, 256 * t:256 * t + 128], T.CF[:], float(lo[t]), A.add, M0, A.mult, rd="CF M0", wr="NR")
-            ts(T.VF[:, 256 * t + 128:256 * t + 256], T.CF[:], float(lo[t]), A.add, rd="CF", wr="VFr")
-        fill(T.BCB[:, 384:512], 0.0, "BCB")
-        for b in range(12):
-            ts(T.BC[:, 32 * b:32 * b + 32], T.NI[:], b, A.arith_shift_right, 1, A.bitwise_and, rd="NI", wr="BC")
-        ts(T.BCB[:, 0:384], T.BC[:], 2.0, A.mult, -1.0, A.add, rd="BC", wr="BCB")
-        for b in range(16):
-            dma("Y", "btd", T.BTD[b], T.BCB[:, 32 * b:32 * b + 32], rd="BCB", wr="BTD")
-        for i in range(8):
-            dma("Y", "bt", T.BT[16 * i:16 * i + 16, :], T.BTD[:], rd="BTD", wr="BT")
-        for p in range(16):
-            dma("Y", "tt", T.TT[p::16, 0:NW], T.TD[:], rd="TD", wr="TTd")
+    def constants3(part):
+        if part == 0:
+            iota(T.ID[:], [[1, NW]], 0, 0, "ID")
+            ts(T.IB[:], T.CF[:], PF, A.is_equal, rd="CF PF", wr="IB")
+            ts(EV, OD, 0.0, A.is_equal, rd="OD", wr="EV")
+            ts(T.NU[:], T.CF[:], PF, A.is_le, -32.0, A.mult, rd="CF PF", wr="NU")
+        elif part == 1:
+            fill(T.ME[:], 0.0, "ME")
+            fill(T.E2[:], 0.0, "E2")
+            fill(T.ML2[:], 1.0, "ML2")
+            fill(T.NR[:], 0.0, "NR")
+            fill(T.MS[:], 0.0, "MS")
+            fill(T.X[:, NW:WN], 0.0, "XL")
+            fill(T.TT[:, NW:WN], 0.0, "TT")
+        else:
+            for t in range(VIS):
+                ts(T.NR[:, 256 * t:256 * t + 128], T.CF[:], float(lo[t]), A.add, M0, A.mult, rd="CF M0", wr="NR")
+                ts(T.VF[:, 256 * t + 128:256 * t + 256], T.CF[:], float(lo[t]), A.add, rd="CF", wr="VFr")
+            for p in range(16):
+                dma("Y", "tt", T.TT[p::16, 0:NW], T.TD[:], rd="TD", wr="TTd")
 
     def kwin():
         return T.KN[:, 0:WN]
 
-    def out(t):
+    def convert(*ii):
+        for i in ii:
+            cp(T.KN[:, 896 * i:896 * i + 896], T.KI[:, 896 * i:896 * i + 896], "KI%d" % i, "KN")
+
+    def out(t, mid, mid2=None):
         a, z = lo[t], lo[t] + 128
         mm(T.ps2[:, 0:128], T.B0[:], T.KN[:, a:z], True, True, "B0 KN", "ps2")
         tt(T.MU[:, 0:128], T.FX[:, a:z], DP[:, 0:128], A.mult, "FX DP", "MUa")
         act(T.FVO[:, 0:128], T.FX[:, a:z], AF.Copy, "FX", "FVO")
         act(T.UM[:], T.KN[:, a:z], AF.Copy, "KN M0", "UM", scale=M0)
+        mid()
         tt(T.MU[:, 128:256], T.ps2[:, 0:128], D, A.mult, "D", "MUb", "ps2")
         scan(T.MS1[:], RS[:], T.MU[:], 0.0, A.mult, A.add, "RS MUa MUb", "MS1")
         cp(T.YL[:], T.MS1[:, 15::16], "MS1", "YL")
+        if mid2:
+            mid2()
         act(T.GO[:], kwin().indirect(T.YL[:, 0:8]), AF.Copy, "KN YL", "GO")
         mm(T.ps2[:, 0:128], T.B0[:], T.GO[:], True, True, "B0 GO", "ps2")
+        act(T.SQ2[:], T.MS1[:, 15::16], AF.Square, "MS1", "SQ2", bias=-a - 63.5)
         act(T.GZ[:], T.GO[:], AF.Copy, "GO NM0", "GZ", scale=NM0)
-        tt(T.MU2[:, 128:256], T.FX[:, 0:WN].indirect(T.YL[:, 8:16]), D, A.mult, "FX YL D", "MU2b")
-        ts(T.SQ[:], T.MS1[:, 15::16], a + 63.5, A.subtract, rd="MS1", wr="SQ")
+        tt(T.MU2[:, 128:256], T.FX[:, 0:WN].indirect(T.YL[:, 8:16]), D, A.mult, "FX FXa YL D", "MU2b")
         tt(T.BO[:, 24 * t:24 * t + 16], T.MS1[:, 15::16], T.DUM[:, 0:16], A.subtract, "MS1 DUM", "BO")
-        tt(T.SQ2[:], T.SQ[:], T.SQ[:], A.mult, "SQ", "SQ2")
         ts(T.NLV[:], T.SQ2[:], 4096.0, A.is_ge, rd="SQ2", wr="NLV")
         tt(T.CO[:, 16:24], T.NLV[:, 0:8], T.NLV[:, 8:16], A.mult, "NLV", "COc")
         tt(T.MU2[:, 0:128], T.ps2[:, 0:128], D, A.mult, "D", "MU2a", "ps2")
@@ -273,59 +282,60 @@ def rank_program(g, core, T, topo):
         tt(T.OF[:, 0:24], T.OF[:, 0:24], T.DUM[:, 0:24], A.add, "OF DUM", "OF")
         cp(T.LO[:], T.OF[:, 0:24], "OF", "LO")
         tt(kwin().indirect(T.LO[:, 0:8]), T.GZ[:], T.UM[:], A.add, "LO GZ UM", "KN")
-        cp(T.FX[:, 0:WN].indirect(T.LO[:, 8:24]), T.FVO[:], "LO FVO FVOr", "FX")
 
     def start(t, rows, rkey):
         tt(T.TM[:], rows, D, A.mult, rkey + " D", "TM")
         scan(T.TS[:], RS[:, 0:128], T.TM[:], 0.0, A.mult, A.add, "RS TM", "TS")
-        i = 16 * (4 * t)
-        cp(T.BL[:, i:i + 8], T.TS[:, 15::16], "TS", "BL%d" % (4 * t))
+        cp(T.BL[:, 64 * t:64 * t + 8], T.TS[:, 15::16], "TS", "BL%d" % (4 * t))
         mm(T.ps6[:, 0:8], T.TM[:], T.R[:], True, True, "TM R", "ps6")
+        act(T.CB8[:], T.ps6[:, 0:8], AF.Identity, "", "CB8", "ps6", bias=8224.5)
 
     def zrep(zz, key):
         for k in range(16):
-            if k < 10:
-                cp(T.ZR[:, k::16], zz, key, "ZRv")
-            else:
-                act(T.ZR[:, k::16], zz, AF.Copy, key, "ZRs")
+            act(T.ZR[:, k::16], zz, AF.Copy, key, "ZR")
 
-    def step(t, s, zz, zkey, wa, wkey):
+    def step(t, s, zz, zkey, wa, wkey, gap):
         q = 4 * t + s
         bl, bk = T.BL[:, 16 * q:16 * q + 8], "BL%d" % q
         vb, vk = (T.ps0, "ps0") if q % 2 == 0 else (T.ps1, "ps1")
+
+        def stay(f, k):
+            act(T.FP[:], f, AF.Identity, k + wkey, "FP", bias=wa)
+            mm(vb[:, 0:272:17], T.IF[:], T.FP[:], False, False, "IF FP", vk)
+
         mm(vb[:, 0:272], T.ONB[:], T.CK[:], True, False, "ONB CK", vk)
         cp(T.KL[:], kwin().indirect(bl), "KN " + bk, "KL")
         act(T.CFR[:], kwin().indirect(bl), AF.Copy, "KN " + bk, "CFR")
         act(T.CHB[:], T.CFR[:], AF.Identity, "CFR", "CHB", bias=8224.5)
         mm(vb[:, 136:272], T.CFR[:], T.PFF[:], False, False, "CFR PFF", vk)
-        if s == 0:
-            act(T.CB8[:], T.ps6[:, 0:8], AF.Identity, "", "CB8", "ps6", bias=8224.5)
-            zrep(zz, zkey)
-            tt(T.TB1[:], T.ps6[:, 0:8], T.CB8[:], A.subtract, "CB8", "TB1", "ps6")
+        if s:
+            stay(T.E[:, 0::16], "E ")
+        for c, (a, z) in enumerate(CH):
+            tt(T.DIFF[:, 16 * a:16 * z], T.XW[:].indirect(T.KL[:, a:z]), T.ZR[:, 16 * a:16 * z], A.subtract, "XW XWp KL ZR", "DF%d" % c)
+            act(T.AB[:, 16 * a:16 * z], T.DIFF[:, 16 * a:16 * z], AF.Abs, "DF%d" % c, "AB%d" % c)
+            if c in PE:
+                a, z = PE[c]
+                for k in range(16):
+                    mm(vb[a:z, k + 1:272:17], T.AB[:, 16 * a + k:16 * z:16], T.WB[:], False, False, "AB%d AB%d WB" % (c, c - (c == 3)), vk)
         tt(T.DFB[:], T.X[:, 0:NW].indirect(bl), zz, A.subtract, "X XL " + bk + " " + zkey, "DFB")
+        act(T.ABB[:], T.DFB[:], AF.Abs, "DFB", "ABB")
         if s == 0:
+            tt(T.TB1[:], T.ps6[:, 0:8], T.CB8[:], A.subtract, "CB8", "TB1", "ps6")
             act(T.FF[:, 0:8], T.CB8[:], AF.Identity, "CB8", "FF", scale=1.0 / 64, bias=-161.0)
             act(T.FF[:, 8:16], T.TB1[:], AF.Identity, "TB1", "FF", bias=8224.0)
-        act(T.ABB[:], T.DFB[:], AF.Abs, "DFB", "ABB")
+        gap()
         mm(vb[:, 0:272:17], T.ABB[:], T.WB[:], False, False, "ABB WB", vk)
-        for c, (a, z) in enumerate(CH):
-            tt(T.DIFF[:, 16 * a:16 * z], T.XW[:].indirect(T.KL[:, a:z]), T.ZR[:, 16 * a:16 * z], A.subtract, "XW KL ZRv ZRs", "DF%d" % c)
-            act(T.AB[:, 16 * a:16 * z], T.DIFF[:, 16 * a:16 * z], AF.Abs, "DF%d" % c, "AB%d" % c)
-            for k in range(16):
-                mm(vb[a:z, k + 1:272:17], T.AB[:, 16 * a + k:16 * z:16], T.WB[:], False, False, "AB%d WB" % c, vk)
-            if c == 1:
-                act(T.FP[:], T.FF[:], AF.Identity, "FF " + wkey, "FP", bias=wa)
-                mm(vb[:, 0:272:17], T.IF[:], T.FP[:], False, False, "IF FP", vk)
+        if s == 0:
+            stay(T.FF[:], "FF ")
         mm(vb[:, 0:272], T.CHB[:], T.PB[:], False, True, "CHB PB", vk)
         scan(T.VM[:], T.R0[:], vb[:, 0:272], 1.0e9, A.max, A.min, "R0", "VM", vk)
         ts(T.RR[:], T.VM[:, 16::17], M7, A.add, M7, A.subtract, rd="VM", wr="RR")
-        tt(T.FF[:], T.VM[:, 16::17], T.RR[:], A.subtract, "VM RR", "FF")
-        ts(T.T1[:], T.FF[:, 0:8], 64.0, A.mult, 2080.0, A.add, rd="FF", wr="T1")
-        tt(T.E[:, 0::16], T.T1[:], T.FF[:, 8:16], A.add, "T1 FF", "E")
-        scan(T.HO[:], RS[:, 0:128], T.E[:], 0.0, A.mult, A.add, "RS E", "HO")
-        tt(T.EM[:], T.HO[:], DP[:, 0:128], A.mult, "HO DP", "EM")
-        mm(T.ps6[:, 0:8], T.EM[:], T.R[:], True, True, "EM R", "ps6")
-        cp(T.BL[:, 16 * q + 16:16 * q + 24], T.ps6[:, 0:8], "", "BL%d" % (q + 1), "ps6")
+        tt(T.E[:, 0::16], T.VM[:, 16::17], T.RR[:], A.subtract, "VM RR", "E")
+        scan(T.HO[:], T.RSB[:], T.E[:], 0.0, A.mult, A.add, "RSB E", "HO")
+        tt(T.EM[:], T.HO[:], DP[:, 0:256], A.mult, "HO DP", "EM")
+        mm(T.ps6[:, 0:8], T.EM[:, 0:128], T.RB64[:], True, False, "EM RB64", "ps6")
+        mm(T.ps6[:, 0:8], T.EM[:, 128:256], T.RB[:], False, True, "EM RB", "ps6")
+        ts(T.BL[:, 16 * q + 16:16 * q + 24], T.ps6[:, 0:8], 2080.0, A.add, wr="BL%d" % (q + 1), ps="ps6")
 
     def seat(t, zz, zkey):
         fin = t == VIS - 1
@@ -342,6 +352,8 @@ def rank_program(g, core, T, topo):
         mm(T.ps2[:, 0:128], T.B0[:], T.VK[:, 128:256], True, True, "B0 VKb", "ps2")
         act(T.CDE[:], T.BT[:].indirect(bl), AF.Copy, "BT EV " + bk, "CDE", scale=EV)
         act(T.CDO[:], T.BT[:].indirect(bl), AF.Copy, "BT OD " + bk, "CDO", scale=OD)
+        ts(T.BLF[:], T.ps6[:, 0:8], 2080.0, A.add, wr="BLF", ps="ps6")
+        act(T.SQ2[:, 0:8], T.BLF[:], AF.Square, "BLF", "SQ2", bias=-a - 63.5)
         for h in range(2):
             ps, pk = (T.ps3, "ps3") if h == 0 else (T.ps4, "ps4")
             for i in range(4):
@@ -358,17 +370,13 @@ def rank_program(g, core, T, topo):
         ts(zn, T.ZQ[:], -M0C, A.add, rd="ZQ", wr=znk)
         if not fin:
             send(nxt, T.ZL[:, 128 * t:128 * t + 128], zn, "aZ%d" % t, znk)
-        cp(T.BLF[:], T.ps6[:, 0:8], "", "BLF", "ps6")
-        ts(T.SQ[:, 0:8], T.BLF[:], a + 63.5, A.subtract, rd="BLF", wr="SQ")
         tt(T.MU[:, 0:128], T.ps2[:, 0:128], D, A.mult, "D", "MUa", "ps2")
-        tt(T.SQ2[:, 0:8], T.SQ[:, 0:8], T.SQ[:, 0:8], A.mult, "SQ", "SQ2")
         scan(T.MS1[:, 0:128], RS[:, 0:128], T.MU[:, 0:128], 0.0, A.mult, A.add, "RS MUa", "MS1")
         ts(T.NLV[:, 0:8], T.SQ2[:, 0:8], 4096.0, A.is_ge, rd="SQ2", wr="NLV")
         cp(T.VL[:], T.MS1[:, 15:128:16], "MS1", "VL")
         tt(T.ME[:, 0::16], T.NLV[:, 0:8], T.CO[:, 16:24], A.mult, "NLV COc", "ME")
-        tt(T.MAY[:], T.NLV[:, 0:8], T.CO[:, 16:24], A.mult, "NLV COc", "MAY")
         scan(T.MH[:], T.RSB[:, 0:128], T.ME[:], 0.0, A.mult, A.add, "RSB ME", "MH")
-        tt(T.MU2[:, 0:128], T.FX[:, 0:WN].indirect(T.VL[:]), D, A.mult, "FX VL D", "MU2a")
+        tt(T.MU2[:, 0:128], T.FX[:, 0:WN].indirect(T.VL[:]), D, A.mult, "FX FXa VL D", "MU2a")
         tt(T.MX[:], T.MH[:], DP[:, 0:128], A.mult, "MH DP", "MX")
         mm(T.ps5[:, 0:8], T.MX[:], T.RB[:], True, True, "MX RB", "ps5")
         scan(T.MS2[:, 0:128], RS[:, 0:128], T.MU2[:, 0:128], 0.0, A.mult, A.add, "RS MU2a", "MS2")
@@ -390,8 +398,8 @@ def rank_program(g, core, T, topo):
         tt(T.EM2[:], T.H2[:], DP[:, 0:256], A.mult, "H2 DP", "EM2")
         mm(T.ps5[:, 32:40], T.EM2[:, 0:128], T.RB[:], True, True, "EM2 RB", "ps5")
         mm(T.ps5[:, 40:48], T.EM2[:, 128:256], T.RB[:], True, True, "EM2 RB", "ps5")
-        tt(T.CND[:, 0:8], T.ps5[:, 32:40], T.MAY[:], A.mult, "MAY", "CN0", "ps5")
-        tt(T.CND[:, 8:16], T.ps5[:, 32:40], T.MAY[:], A.mult, "MAY", "CN1", "ps5")
+        tt(T.CND[:, 0:8], T.ps5[:, 32:40], T.ME[:, 0::16], A.mult, "ME", "CN0", "ps5")
+        tt(T.CND[:, 8:16], T.ps5[:, 32:40], T.ME[:, 0::16], A.mult, "ME", "CN1", "ps5")
         cp(T.CND[:, 24:32], T.ps5[:, 40:48], "", "CN3", "ps5")
         tt(T.CND[:, 16:24], T.CE[:, 0:8], T.CND[:, 0:8], A.mult, "CE CN0", "CN2")
         if not fin:
@@ -403,39 +411,42 @@ def rank_program(g, core, T, topo):
         if not fin:
             m0 = 16 * t
             cp(T.MS[:, m0:m0 + 8], T.OF[:, 24:32], "OF", "MS")
-            op("V", lambda: g.vector.tensor_reduce(out=T.AS[:, 0:1], in_=T.ps5[:, 48:56], axis=AxisListType.X, op=A.add), "", "AS", "ps5")
-            cp(T.AI[:, 0:1], T.AS[:, 0:1], "AS", "AI0")
-            ts(T.AI[:, 1:2], T.AI[:, 0:1], 31, A.bitwise_and, rd="AI0", wr="AI1")
-            ts(T.MS[:, m0 + 8:m0 + 9], T.AI[:, 1:2], WT, A.mult, rd="AI1", wr="MS")
-            send(nxt, T.ML[:, m0:m0 + 16], T.MS[:, m0:m0 + 16], "aM%d" % t, "MS")
+            act(T.AQ[:], T.ps5[:, 48:56], AF.Copy, "", "AQ MSa", "ps5", accum_out=T.MS[:, m0 + 8:m0 + 9])
+            send(nxt, T.ML[:, m0:m0 + 16], T.MS[:, m0:m0 + 16], "aM%d" % t, "MS MSa")
             if t == 2:
                 cp(T.L8[:], T.OF[:, 24:32], "OF", "L8")
+            arrives("aC%d" % t, "CL%d" % t)
+            arrives("aZ%d" % t, "ZL%d" % t)
+            arrives("aM%d" % t, "M%d" % t)
+            zrep(T.ZL[:, 128 * t:128 * t + 128], "ZL%d" % t)
         tt(kwin().indirect(T.LS[:, 0:16]), T.VK[:], T.NR[:, 256 * t:256 * t + 256], A.add, "LS VKa VKb NR", "KN")
         cp(T.FX[:, 0:WN].indirect(T.LS[:, 8:24]), vf, "LS VF%d VFr" % t, "FX")
         cp(T.X[:].indirect(T.LS[:, 8:16]), zn, "LS " + znk, "X XL")
         if not fin:
             act(T.XW[:, a:a + 128], T.X[:, a:a + 128], AF.Copy, "X", "XW")
 
+    def gap(t, s):
+        if t == 0:
+            constants3(s)
+        elif s == 0:
+            cp(T.AI[:, 0:1], T.ML[:, 16 * t - 8:16 * t - 7], "M%d" % (t - 1), "AI0")
+            ts(T.AI[:, 1:2], T.AI[:, 0:1], 31, A.bitwise_and, rd="AI0", wr="AI1")
+            ts(T.WAQ[:, 0:1], T.AI[:, 1:2], WT, A.mult, rd="AI1", wr="WA")
+        if s == 0:
+            cp(T.FX[:, 0:WN].indirect(T.LO[:, 8:24]), T.FVO[:], "LO FVO FVOr", "FX")
+
     fill(T.FVO[:, 128:256], float(NW), "FVOr")
-    constants2()
-    out(0)
-    start(0, T.BI[:], "BI")
-    fill(T.XW[:, lo[0]:lo[0] + 128], 4096.0, "XW")
+    zrep(T.Z0[:], "Z0")
+    convert(3, 2)
+    out(0, lambda: start(0, T.BI[:], "BI"), lambda: convert(0, 1))
+    fill(T.XW[:, lo[0]:lo[0] + 128], 4096.0, "XWp")
     for t in range(VIS):
         if t == 0:
             zz, zkey, wa, wkey = T.Z0[:], "Z0", WA0, "WA0"
         else:
-            u = t - 1
-            arrives("aC%d" % u, "CL%d" % u)
-            arrives("aZ%d" % u, "ZL%d" % u)
-            arrives("aM%d" % u, "M%d" % u)
-            zz, zkey = T.ZL[:, 128 * u:128 * u + 128], "ZL%d" % u
-            wa, wkey = T.ML[:, 16 * u + 8:16 * u + 9], "M%d" % u
-            start(t, T.TT[:].indirect(T.CL[:, 16 * u:16 * u + 8]), "TT TTd CL%d" % u)
+            zz, zkey, wa, wkey = T.ZL[:, 128 * t - 128:128 * t], "ZL%d" % (t - 1), T.WAQ[:, 0:1], "WA"
         for s in range(ST):
-            step(t, s, zz, zkey, wa, wkey)
-            if t == 0 and s == 0:
-                constants3()
+            step(t, s, zz, zkey, wa, wkey, lambda: gap(t, s))
         seat(t, zz, zkey)
         if t == 2:
             dma("Y", "tb", T.TB[:], T.TT[0::16, 0:NW], rd="TT", wr="TB")
@@ -443,8 +454,8 @@ def rank_program(g, core, T, topo):
             arrives("aTB", "TBL")
             dma("Y", "ot", T.OT[0::16, 0:NW], T.TBL[:], rd="TBL", wr="OT")
         if t < VIS - 1:
-            fill(T.XW[:, lo[t + 1]:lo[t + 1] + 128], 4096.0, "XW")
-            out(t + 1)
+            fill(T.XW[:, lo[t + 1]:lo[t + 1] + 128], 4096.0, "XWp")
+            out(t + 1, lambda: start(t + 1, T.TT[:].indirect(T.CL[:, 16 * t:16 * t + 8]), "TT TTd CL%d" % t))
     arrives("aB", "CLB")
     act(T.OR[:], T.ID[:].indirect(T.CL[:, 48:56]), AF.Copy, "ID CLB", "OR")
     dma("Y", "out", T.yz[:], T.ZN[:, 384:512], rd="ZN3")

from concourse.mybir import AluOpType as A, ActivationFunctionType as AF

NW, NB, NJ, VIS, ST = 3584, 2560, 1024, 4, 3
WN = 3856
DA, DB = 3600, 3728
WT = 2176.0
M7, M0C = 1.5 * 2.0 ** 30, 1.5 * 2.0 ** 23
CH = [(0, 64), (64, 96), (96, 112), (112, 128)]
PE = {0: (0, 64), 1: (64, 96), 3: (96, 128)}
BUFS = {
    "float32": "KN:3856 FX:3856 TT:3856 OT:3856 ID:3584 TRF:224 ML:48 MS:48 COLF:16 CF:128 C15F:128 CGF:128 D:128 B0:128 R:8 IF:128 GI:136 "
               "PFF:136 R0:272 RS:256 I8:8 J8:8 DUM:40 NN:64 BO:96 BSS:128 NR:1024 VF:1024 FVO:256 CFR:128 FP:16 VM:272 RR:16 FF:16 "
               "TM:128 TS:128 TB1:8 MU:256 MS1:256 GO:128 GZ:128 UM:128 MU2:256 MS2:256 SQ2:16 NLV:16 CE:16 "
               "CO:24 OF:32 BLF:8 ZS:128 ZQ:128 VK:256 CND:32 AQ:8 WAQ:4 OR:128",
    "bfloat16": "X:3856 XW:3584 BT:4096 Z0:128 ZL:384 ZN:512 ZR:2048 RB:8 RB64:8 E:256 HO:256 EM:256 IB:128 ONB:128 WB:16 NU:128 PB:272 "
                "CK:272 RSB:256 BCB:1024 DIFF:2048 AB:2048 DFB:128 ABB:128 CHB:128 CB8:8 CDE:128 CDO:128 ME:128 MH:128 MX:128 ML2:16 "
                "EQ:1024 E2:256 H2:256 EM2:256 LA:8",
    "int32": "KI:3584 FI:1024 BI:128 TRI:224 CI:128 C15:128 CG:128 COLI:4 NI:64 BC:768 AI:4",
    "uint16": "CL:64 BL:320 KL:128 YL:16 LO:24 VL:8 LS:32 L8:8",
}
SCRATCH = {"TD": ("dram", [128, 224], "float32"), "TB": ("dram", [128, 224], "float32"), "TBL": ("dram", [128, 224], "float32"),
           "BTD": ("dram", [16, 64, 64], "bfloat16")}
for _d in BUFS:
    for _b in BUFS[_d].split():
        SCRATCH[_b.split(":")[0]] = ("sbuf", [128, int(_b.split(":")[1])], _d)
for _i in range(8):
    SCRATCH["ps%d" % _i] = ("psum", [128, 512], "float32")
SEMAPHORES = ["V", "S", "P", "G", "kn0", "kn1", "kn2", "kn3", "lx", "lw", "lf", "lb", "lz", "lt", "btd", "bt", "tt", "tb", "ot", "out",
              "aT", "aB", "aTB", "loc"] + ["a%s%d" % (k, t) for k in "CZM" for t in range(3)]


def rank_program(g, core, T, topo):
    rank = T.rank_of(core)
    if rank is None:
        return
    cores = T.cores
    n = len(cores)
    Q = {"V": g.vector, "S": g.scalar, "P": g.tensor, "G": g, "Y": g.sync}
    tot, waited, last, readers, excl = {}, {}, {}, {}, {}

    def need(eng, sem, val):
        val = tot[sem] if val is None else val
        if waited.get((eng, sem), 0) < val:
            Q[eng].wait_ge(T.sem[sem], val)
            waited[(eng, sem)] = val

    def before(eng, rd, wr, ps):
        for k in rd:
            if k in last:
                need(eng, last[k][0], last[k][1])
        for k in wr:
            if k in last:
                need(eng, last[k][0], last[k][1])
            for s, v in readers.get(k, {}).items():
                if s != eng:
                    need(eng, s, v)
        for k in ps:
            for s, v in excl.get(k, {}).items():
                if s != eng:
                    need(eng, s, v)

    def after(sem, val, rd, wr, ps):
        for k in rd:
            readers.setdefault(k, {})[sem] = val
        for k in wr:
            last[k] = (sem, val)
            readers[k] = {}
        for k in ps:
            excl.setdefault(k, {})[sem] = val

    def op(eng, fn, rd, wr, ps):
        rd, wr, ps = rd.split(), wr.split(), ps.split()
        before(eng, rd, wr, ps)
        fn().then_inc(T.sem[eng], 1)
        tot[eng] = tot.get(eng, 0) + 1
        after(eng, tot[eng], rd, wr, ps)

    def ts(out, in0, s1, op0, s2=None, op1=None, rd="", wr="", ps=""):
        if op1 is None:
            op("V", lambda: g.vector.tensor_scalar(out=out, in0=in0, scalar1=s1, scalar2=None, op0=op0), rd, wr, ps)
        else:
            op("V", lambda: g.vector.tensor_scalar(out=out, in0=in0, scalar1=s1, scalar2=s2, op0=op0, op1=op1), rd, wr, ps)

    def tt(out, in0, in1, o, rd="", wr="", ps=""):
        op("V", lambda: g.vector.tensor_tensor(out=out, in0=in0, in1=in1, op=o), rd, wr, ps)

    def cp(out, in_, rd="", wr="", ps=""):
        op("V", lambda: g.vector.tensor_copy(out=out, in_=in_), rd, wr, ps)

    def scan(out, d0, d1, init, o0, o1, rd="", wr="", ps=""):
        op("V", lambda: g.vector.tensor_tensor_scan(out=out, data0=d0, data1=d1, initial=init, op0=o0, op1=o1), rd, wr, ps)

    def fill(ap, c, wr):
        op("V", lambda: g.vector.memset(ap, c), "", wr, "")

    def act(out, in_, f, rd="", wr="", ps="", **kw):
        op("S", lambda: g.scalar.activation(out=out, in_=in_, func=f, **kw), rd, wr, ps)

    def mm(out, l, r, a, z, rd="", ps=""):
        op("P", lambda: g.tensor.matmul(out=out, lhsT=l, rhs=r, start=a, stop=z), rd, "", ps)

    def iota(out, pat, base, cm, wr, flag=True):
        if flag:
            op("G", lambda: g.iota(out=out, pattern=pat, base=base, channel_multiplier=cm, allow_small_or_imprecise_dtypes=True), "", wr, "")
        else:
            op("G", lambda: g.iota(out=out, pattern=pat, base=base, channel_multiplier=cm), "", wr, "")

    def dma(eng, grp, out, in_, rd="", wr=""):
        rd, wr = rd.split(), wr.split()
        for k in rd:
            if k in last:
                need(eng, last[k][0], last[k][1])
        for k in wr:
            if k in last and last[k][0] != grp:
                need(eng, last[k][0], last[k][1])
            for s, v in readers.get(k, {}).items():
                need(eng, s, v)
        Q[eng].dma_start(out=out, in_=in_).then_inc(T.sem[grp], 16)
        tot[grp] = tot.get(grp, 0) + 16
        after(grp, None, rd, wr, [])

    def send(dst, out, in_, sem, rd):
        before("G", rd.split(), [], [])
        rid, pid, _ = topo.addr(dst)
        m = 0
        for e in topo.engines(core, dst)[:8]:
            m |= 1 << e
        g.remote_dma(out, in_, T.sem[sem], T.sem.loc, pid, rid, m)
        tot["loc"] = tot.get("loc", 0) + 8

    def arrives(sem, key):
        tot[sem] = 8
        last[key] = (sem, 8)
        readers[key] = {}

    nxt, prv = cores[(rank + 1) % n], cores[(rank - 1) % n]
    lo = [NB + 128 * ((rank - t) % n) for t in range(VIS)]
    D, RS, DP = T.D[:], T.RS, T.ps7
    PF, P15, PG, PP, OD, EV, M0, NM0, WA0 = [T.COLF[:, i:i + 1] for i in range(9)]
    PI, P15I, PGI, PEI = [T.COLI[:, i:i + 1] for i in range(4)]

    for i in (3, 2, 0, 1):
        dma("Y", "kn%d" % i, T.KI[:, 896 * i:896 * i + 896], T.kn[:, 896 * i:896 * i + 896], wr="KI%d" % i)
    for p in range(16):
        dma("S", "lf", T.FI[p::16, :], T.ft[:], wr="FI")
    dma("S", "lt", T.TRI[:], T.tr[:], wr="TRI")
    dma("Y", "lx", T.X[:, 0:NW], T.x0[:], wr="XL")
    for p in range(16):
        dma("S", "lb", T.BI[p::16, :], T.bs[:], wr="BI")
    dma("S", "lz", T.Z0[:], T.z0[:], wr="Z0")
    dma("Y", "lw", T.XW[:], T.x0[:], wr="XW")

    iota(T.NI[0:64, :], [[1, 64]], 0, 64, "NI", False)
    fill(T.CK[:], 0.0, "CK")
    iota(T.CK[0:1, :], [[0, 16], [128, 17]], 0, 0, "CK")
    iota(T.CI[:], [[1, 128]], 0, 0, "CI", False)
    iota(PI, [[0, 1]], 0, 1, "PI", False)
    iota(T.CF[:], [[1, 128]], 0, 0, "CF")
    iota(PF, [[0, 1]], 0, 1, "PF")
    iota(T.I8[:], [[16, 8]], 0, 0, "I8")
    iota(T.GI[:], [[17, 8], [1, 17]], 0, 0, "GI")
    fill(T.BCB[0:64, 768:1024], 0.0, "BCB")
    for b in range(12):
        ts(T.BC[0:64, 64 * b:64 * b + 64], T.NI[0:64, :], b, A.arith_shift_right, 1, A.bitwise_and, rd="NI", wr="BC")
    ts(T.BCB[0:64, 0:768], T.BC[0:64, :], 2.0, A.mult, -1.0, A.add, rd="BC", wr="BCB")
    for b in range(16):
        dma("Y", "btd", T.BTD[b], T.BCB[0:64, 64 * b:64 * b + 64], rd="BCB", wr="BTD")
    for i in range(8):
        dma("Y", "bt", T.BT[16 * i:16 * i + 16, :], T.BTD[:], rd="BTD", wr="BT")
    iota(T.FX[:, 0:NB], [[0, NB]], -1, 0, "FXa")
    ts(P15I, PI, 15, A.bitwise_and, rd="PI", wr="P15I")
    ts(PGI, PI, 4, A.arith_shift_right, rd="PI", wr="PGI")
    ts(T.C15[:], T.CI[:], 15, A.bitwise_and, rd="CI", wr="C15")
    ts(T.CG[:], T.CI[:], 4, A.arith_shift_right, rd="CI", wr="CG")
    ts(PEI, PI, 4, A.arith_shift_right, 1, A.bitwise_and, rd="PI", wr="PEI")
    cp(P15, P15I, "P15I", "P15")
    cp(PG, PGI, "PGI", "PG")
    cp(T.C15F[:], T.C15[:], "C15", "C15F")
    cp(T.CGF[:], T.CG[:], "CG", "CGF")
    cp(OD, PEI, "PEI", "OD")
    ts(T.D[:], T.C15F[:], P15, A.is_equal, rd="C15F P15", wr="D")
    ts(M0, P15, 0.0, A.is_equal, rd="P15", wr="M0")
    ts(NM0, P15, 0.0, A.not_equal, rd="P15", wr="NM0")
    ts(T.B0[:], T.CGF[:], PG, A.is_equal, M0, A.mult, rd="CGF PG M0", wr="B0")
    cp(DP[:, 0:128], D, "D", "DP")
    cp(DP[:, 128:256], D, "D", "DP")
    fill(T.RS[:], 1.0, "RS")
    fill(T.RS[:, 0::16], 0.0, "RS")
    ts(T.J8[:], T.I8[:], P15, A.add, rd="I8 P15", wr="J8")
    for i, d in enumerate((DA, DA, DB, DA, DA)):
        ts(T.DUM[:, 8 * i:8 * i + 8], T.J8[:], float(d), A.add, rd="J8", wr="DUM")
    for t in range(VIS):
        ts(T.NN[:, 16 * t:16 * t + 8], T.J8[:], float(lo[t]), A.add, rd="J8", wr="NN")
        ts(T.NN[:, 16 * t + 8:16 * t + 16], T.J8[:], float(lo[t]), A.add, rd="J8", wr="NN")
        fill(T.BO[:, 24 * t + 16:24 * t + 24], float(lo[t] - DB), "BO")
        fill(T.BSS[:, 32 * t + 8:32 * t + 16], float(lo[t] - DB), "BSS")
    fill(T.FX[:, NW:WN], -1.0, "FX")
    fill(T.KN[:, NW:WN], -1.0, "KN")
    cp(T.FX[:, NB:NW], T.FI[:], "FI", "FX")
    cp(T.TRF[:], T.TRI[:], "TRI", "TRF")
    ts(T.IF[:], T.CF[:], PF, A.is_equal, rd="CF PF", wr="IF")
    ts(T.R[:], T.CGF[:, 0::16], PG, A.is_equal, rd="CGF PG", wr="R")
    cp(T.RB[:], T.R[:], "R", "RB")
    ts(T.RB64[:], T.R[:], 64.0, A.mult, rd="R", wr="RB64")
    fill(T.RSB[:], 1.0, "RSB")
    fill(T.RSB[:, 0::16], 0.0, "RSB")
    ts(T.WB[:, 0:8], T.R[:], WT, A.mult, rd="R", wr="WB")
    ts(T.WB[:, 8:16], T.R[:], WT, A.mult, rd="R", wr="WB")
    fill(T.ONB[:], 1.0, "ONB")
    tt(PP, PF, PG, A.add, "PF PG", "PP0")
    ts(PP, PP, 1.0, A.add, rd="PP0", wr="PP")
    ts(T.PB[:, 0:136], T.GI[:], PP, A.is_equal, 1.0 / 64, A.mult, rd="GI PP", wr="PB")
    ts(T.PB[:, 136:272], T.GI[:], PP, A.is_equal, -1.0, A.mult, rd="GI PP", wr="PB")
    ts(T.PFF[:], T.GI[:], PP, A.is_equal, rd="GI PP", wr="PFF")
    fill(T.CK[32:33, 0:136], -161.0, "CK")
    fill(T.CK[32:33, 136:272], 8192.0, "CK")
    fill(T.CK[64:65, 136:272], 32.0, "CK")
    fill(T.CK[32:33, 0::17], 0.0, "CK")
    fill(T.CK[64:65, 0::17], 0.0, "CK")
    fill(T.R0[:], -1.0e9, "R0")
    fill(T.R0[:, 0::17], 1.0e9, "R0")
    fill(T.E[:], 0.0, "E")
    fill(WA0, 0.0, "WA0")
    send(nxt, T.TD[:], T.TRF[:], "aT", "TRF")
    arrives("aT", "TD")
    last["XWp"] = last["XW"]

    def constants3(part):
        if part == 0:
            iota(T.ID[:], [[1, NW]], 0, 0, "ID")
            ts(T.IB[:], T.CF[:], PF, A.is_equal, rd="CF PF", wr="IB")
            ts(EV, OD, 0.0, A.is_equal, rd="OD", wr="EV")
            ts(T.NU[:], T.CF[:], PF, A.is_le, -32.0, A.mult, rd="CF PF", wr="NU")
        elif part == 1:
            fill(T.ME[:], 0.0, "ME")
            fill(T.E2[:], 0.0, "E2")
            fill(T.ML2[:], 1.0, "ML2")
            fill(T.NR[:], 0.0, "NR")
            fill(T.MS[:], 0.0, "MS")
            fill(T.X[:, NW:WN], 0.0, "XL")
            fill(T.TT[:, NW:WN], 0.0, "TT")
        else:
            for t in range(VIS):
                ts(T.NR[:, 256 * t:256 * t + 128], T.CF[:], float(lo[t]), A.add, M0, A.mult, rd="CF M0", wr="NR")
                ts(T.VF[:, 256 * t + 128:256 * t + 256], T.CF[:], float(lo[t]), A.add, rd="CF", wr="VFr")
            for p in range(16):
                dma("Y", "tt", T.TT[p::16, 0:NW], T.TD[:], rd="TD", wr="TTd")

    def kwin():
        return T.KN[:, 0:WN]

    def convert(*ii):
        for i in ii:
            cp(T.KN[:, 896 * i:896 * i + 896], T.KI[:, 896 * i:896 * i + 896], "KI%d" % i, "KN")

    def out(t, mid, mid2=None):
        a, z = lo[t], lo[t] + 128
        mm(T.ps2[:, 0:128], T.B0[:], T.KN[:, a:z], True, True, "B0 KN", "ps2")
        tt(T.MU[:, 0:128], T.FX[:, a:z], DP[:, 0:128], A.mult, "FX DP", "MUa")
        act(T.FVO[:, 0:128], T.FX[:, a:z], AF.Copy, "FX", "FVO")
        act(T.UM[:], T.KN[:, a:z], AF.Copy, "KN M0", "UM", scale=M0)
        mid()
        tt(T.MU[:, 128:256], T.ps2[:, 0:128], D, A.mult, "D", "MUb", "ps2")
        scan(T.MS1[:], RS[:], T.MU[:], 0.0, A.mult, A.add, "RS MUa MUb", "MS1")
        cp(T.YL[:], T.MS1[:, 15::16], "MS1", "YL")
        if mid2:
            mid2()
        act(T.GO[:], kwin().indirect(T.YL[:, 0:8]), AF.Copy, "KN YL", "GO")
        mm(T.ps2[:, 0:128], T.B0[:], T.GO[:], True, True, "B0 GO", "ps2")
        act(T.SQ2[:], T.MS1[:, 15::16], AF.Square, "MS1", "SQ2", bias=-a - 63.5)
        act(T.GZ[:], T.GO[:], AF.Copy, "GO NM0", "GZ", scale=NM0)
        tt(T.MU2[:, 128:256], T.FX[:, 0:WN].indirect(T.YL[:, 8:16]), D, A.mult, "FX FXa YL D", "MU2b")
        tt(T.BO[:, 24 * t:24 * t + 16], T.MS1[:, 15::16], T.DUM[:, 0:16], A.subtract, "MS1 DUM", "BO")
        ts(T.NLV[:], T.SQ2[:], 4096.0, A.is_ge, rd="SQ2", wr="NLV")
        tt(T.CO[:, 16:24], T.NLV[:, 0:8], T.NLV[:, 8:16], A.mult, "NLV", "COc")
        tt(T.MU2[:, 0:128], T.ps2[:, 0:128], D, A.mult, "D", "MU2a", "ps2")
        scan(T.MS2[:], RS[:], T.MU2[:], 0.0, A.mult, A.add, "RS MU2a MU2b", "MS2")
        tt(T.CE[:], T.MS2[:, 15::16], T.NN[:, 16 * t:16 * t + 16], A.is_equal, "MS2 NN", "CE")
        tt(T.CO[:, 0:8], T.CE[:, 0:8], T.CO[:, 16:24], A.mult, "CE COc", "COa")
        tt(T.CO[:, 8:16], T.CE[:, 8:16], T.CO[:, 0:8], A.mult, "CE COa", "COb")
        tt(T.OF[:, 0:24], T.CO[:], T.BO[:, 24 * t:24 * t + 24], A.mult, "COa COb COc BO", "OF")
        tt(T.OF[:, 0:24], T.OF[:, 0:24], T.DUM[:, 0:24], A.add, "OF DUM", "OF")
        cp(T.LO[:], T.OF[:, 0:24], "OF", "LO")
        tt(kwin().indirect(T.LO[:, 0:8]), T.GZ[:], T.UM[:], A.add, "LO GZ UM", "KN")

    def start(t, rows, rkey):
        tt(T.TM[:], rows, D, A.mult, rkey + " D", "TM")
        scan(T.TS[:], RS[:, 0:128], T.TM[:], 0.0, A.mult, A.add, "RS TM", "TS")
        cp(T.BL[:, 64 * t:64 * t + 8], T.TS[:, 15::16], "TS", "BL%d" % (4 * t))
        mm(T.ps6[:, 0:8], T.TM[:], T.R[:], True, True, "TM R", "ps6")
        act(T.CB8[:], T.ps6[:, 0:8], AF.Identity, "", "CB8", "ps6", bias=8224.5)

    def zrep(zz, key):
        for k in range(16):
            act(T.ZR[:, k::16], zz, AF.Copy, key, "ZR")

    def step(t, s, zz, zkey, wa, wkey, gap):
        q = 4 * t + s
        bl, bk = T.BL[:, 16 * q:16 * q + 8], "BL%d" % q
        vb, vk = (T.ps0, "ps0") if q % 2 == 0 else (T.ps1, "ps1")

        def stay(f, k):
            act(T.FP[:], f, AF.Identity, k + wkey, "FP", bias=wa)
            mm(vb[:, 0:272:17], T.IF[:], T.FP[:], False, False, "IF FP", vk)

        mm(vb[:, 0:272], T.ONB[:], T.CK[:], True, False, "ONB CK", vk)
        cp(T.KL[:], kwin().indirect(bl), "KN " + bk, "KL")
        act(T.CFR[:], kwin().indirect(bl), AF.Copy, "KN " + bk, "CFR")
        act(T.CHB[:], T.CFR[:], AF.Identity, "CFR", "CHB", bias=8224.5)
        mm(vb[:, 136:272], T.CFR[:], T.PFF[:], False, False, "CFR PFF", vk)
        if s:
            stay(T.E[:, 0::16], "E ")
        for c, (a, z) in enumerate(CH):
            tt(T.DIFF[:, 16 * a:16 * z], T.XW[:].indirect(T.KL[:, a:z]), T.ZR[:, 16 * a:16 * z], A.subtract, "XW XWp KL ZR", "DF%d" % c)
            act(T.AB[:, 16 * a:16 * z], T.DIFF[:, 16 * a:16 * z], AF.Abs, "DF%d" % c, "AB%d" % c)
            if c in PE:
                a, z = PE[c]
                for k in range(16):
                    mm(vb[a:z, k + 1:272:17], T.AB[:, 16 * a + k:16 * z:16], T.WB[:], False, False, "AB%d AB%d WB" % (c, c - (c == 3)), vk)
        tt(T.DFB[:], T.X[:, 0:NW].indirect(bl), zz, A.subtract, "X XL " + bk + " " + zkey, "DFB")
        act(T.ABB[:], T.DFB[:], AF.Abs, "DFB", "ABB")
        if s == 0:
            tt(T.TB1[:], T.ps6[:, 0:8], T.CB8[:], A.subtract, "CB8", "TB1", "ps6")
            act(T.FF[:, 0:8], T.CB8[:], AF.Identity, "CB8", "FF", scale=1.0 / 64, bias=-161.0)
            act(T.FF[:, 8:16], T.TB1[:], AF.Identity, "TB1", "FF", bias=8224.0)
        gap()
        mm(vb[:, 0:272:17], T.ABB[:], T.WB[:], False, False, "ABB WB", vk)
        if s == 0:
            stay(T.FF[:], "FF ")
        mm(vb[:, 0:272], T.CHB[:], T.PB[:], False, True, "CHB PB", vk)
        scan(T.VM[:], T.R0[:], vb[:, 0:272], 1.0e9, A.max, A.min, "R0", "VM", vk)
        ts(T.RR[:], T.VM[:, 16::17], M7, A.add, M7, A.subtract, rd="VM", wr="RR")
        tt(T.E[:, 0::16], T.VM[:, 16::17], T.RR[:], A.subtract, "VM RR", "E")
        scan(T.HO[:], T.RSB[:], T.E[:], 0.0, A.mult, A.add, "RSB E", "HO")
        tt(T.EM[:], T.HO[:], DP[:, 0:256], A.mult, "HO DP", "EM")
        mm(T.ps6[:, 0:8], T.EM[:, 0:128], T.RB64[:], True, False, "EM RB64", "ps6")
        mm(T.ps6[:, 0:8], T.EM[:, 128:256], T.RB[:], False, True, "EM RB", "ps6")
        ts(T.BL[:, 16 * q + 16:16 * q + 24], T.ps6[:, 0:8], 2080.0, A.add, wr="BL%d" % (q + 1), ps="ps6")

    def seat(t, zz, zkey):
        fin = t == VIS - 1
        a = lo[t]
        q = 4 * t + 3
        bl, bk = T.BL[:, 16 * q:16 * q + 8], "BL%d" % q
        zn, znk = T.ZN[:, 128 * t:128 * t + 128], "ZN%d" % t
        vf = T.VF[:, 256 * t:256 * t + 256]
        if fin:
            send(prv, T.CL[:, 48:56], bl, "aB", bk)
        else:
            send(nxt, T.CL[:, 16 * t:16 * t + 8], bl, "aC%d" % t, bk)
        act(T.VK[:, 128:256], kwin().indirect(bl), AF.Copy, "KN " + bk, "VKb")
        mm(T.ps2[:, 0:128], T.B0[:], T.VK[:, 128:256], True, True, "B0 VKb", "ps2")
        act(T.CDE[:], T.BT[:].indirect(bl), AF.Copy, "BT EV " + bk, "CDE", scale=EV)
        act(T.CDO[:], T.BT[:].indirect(bl), AF.Copy, "BT OD " + bk, "CDO", scale=OD)
        ts(T.BLF[:], T.ps6[:, 0:8], 2080.0, A.add, wr="BLF", ps="ps6")
        act(T.SQ2[:, 0:8], T.BLF[:], AF.Square, "BLF", "SQ2", bias=-a - 63.5)
        for h in range(2):
            ps, pk = (T.ps3, "ps3") if h == 0 else (T.ps4, "ps4")
            for i in range(4):
                gr = 4 * h + i
                r = 32 * (gr // 2)
                cd, ck = (T.CDE, "CDE") if gr % 2 == 0 else (T.CDO, "CDO")
                mm(ps[:, 128 * i:128 * i + 128], T.IB[:], T.NU[:], True, False, "IB NU", pk)
                if i == 2:
                    need("P", "P", tot["P"])
                mm(ps[:, 128 * i:128 * i + 128], cd[r:r + 32, :], cd[r:r + 32, :], False, True, ck, pk)
            act(T.EQ[:, 512 * h:512 * h + 512], ps[:], AF.Relu, "", "EQ%d" % h, pk, bias=-11.0)
        tt(T.ZS[:], T.X[:, 0:NW].indirect(bl), zz, A.add, "X XL " + bk + " " + zkey, "ZS")
        ts(T.ZQ[:], T.ZS[:], 0.4999, A.mult, M0C, A.add, rd="ZS", wr="ZQ")
        ts(zn, T.ZQ[:], -M0C, A.add, rd="ZQ", wr=znk)
        if not fin:
            send(nxt, T.ZL[:, 128 * t:128 * t + 128], zn, "aZ%d" % t, znk)
        tt(T.MU[:, 0:128], T.ps2[:, 0:128], D, A.mult, "D", "MUa", "ps2")
        scan(T.MS1[:, 0:128], RS[:, 0:128], T.MU[:, 0:128], 0.0, A.mult, A.add, "RS MUa", "MS1")
        ts(T.NLV[:, 0:8], T.SQ2[:, 0:8], 4096.0, A.is_ge, rd="SQ2", wr="NLV")
        cp(T.VL[:], T.MS1[:, 15:128:16], "MS1", "VL")
        tt(T.ME[:, 0::16], T.NLV[:, 0:8], T.CO[:, 16:24], A.mult, "NLV COc", "ME")
        scan(T.MH[:], T.RSB[:, 0:128], T.ME[:], 0.0, A.mult, A.add, "RSB ME", "MH")
        tt(T.MU2[:, 0:128], T.FX[:, 0:WN].indirect(T.VL[:]), D, A.mult, "FX FXa VL D", "MU2a")
        tt(T.MX[:], T.MH[:], DP[:, 0:128], A.mult, "MH DP", "MX")
        mm(T.ps5[:, 0:8], T.MX[:], T.RB[:], True, True, "MX RB", "ps5")
        scan(T.MS2[:, 0:128], RS[:, 0:128], T.MU2[:, 0:128], 0.0, A.mult, A.add, "RS MU2a", "MS2")
        cp(T.ML2[:, 0:8], T.ps5[:, 0:8], "", "ML2", "ps5")
        act(vf[:, 0:128], T.ID[:].indirect(bl), AF.Copy, "ID " + bk, "VF%d" % t)
        act(T.VK[:, 0:128], T.VK[:, 128:256], AF.Copy, "VKb NM0", "VKa", scale=NM0)
        for gr in range(8):
            mm(T.ps5[:, 16 + gr:32:8], T.EQ[:, 128 * gr:128 * gr + 128], T.ML2[:, gr::8], True, True, "EQ%d ML2" % (gr // 4), "ps5")
        tt(T.CE[:, 0:8], T.MS2[:, 15:128:16], T.BLF[:], A.is_equal, "MS2 BLF", "CE")
        b0 = 32 * t
        tt(T.BSS[:, b0:b0 + 8], T.BLF[:], T.DUM[:, 0:8], A.subtract, "BLF DUM", "BSS")
        tt(T.BSS[:, b0 + 16:b0 + 24], T.MS1[:, 15:128:16], T.DUM[:, 0:8], A.subtract, "MS1 DUM", "BSS")
        tt(T.BSS[:, b0 + 24:b0 + 32], T.BLF[:], T.DUM[:, 0:8], A.subtract, "BLF DUM", "BSS")
        if t in (1, 2):
            cp(T.L8[:], T.ML[:, 16 * (t - 1):16 * (t - 1) + 8], "M%d" % (t - 1), "L8")
            cp(T.TT[:].indirect(T.L8[:]), vf[:, 0:128], "L8 VF%d" % t, "TT TTd")
        ts(T.E2[:, 0::16], T.ps5[:, 16:32], 0.0, A.is_equal, rd="", wr="E2", ps="ps5")
        scan(T.H2[:], T.RSB[:], T.E2[:], 0.0, A.mult, A.add, "RSB E2", "H2")
        tt(T.EM2[:], T.H2[:], DP[:, 0:256], A.mult, "H2 DP", "EM2")
        mm(T.ps5[:, 32:40], T.EM2[:, 0:128], T.RB[:], True, True, "EM2 RB", "ps5")
        mm(T.ps5[:, 40:48], T.EM2[:, 128:256], T.RB[:], True, True, "EM2 RB", "ps5")
        tt(T.CND[:, 0:8], T.ps5[:, 32:40], T.ME[:, 0::16], A.mult, "ME", "CN0", "ps5")
        tt(T.CND[:, 8:16], T.ps5[:, 32:40], T.ME[:, 0::16], A.mult, "ME", "CN1", "ps5")
        cp(T.CND[:, 24:32], T.ps5[:, 40:48], "", "CN3", "ps5")
        tt(T.CND[:, 16:24], T.CE[:, 0:8], T.CND[:, 0:8], A.mult, "CE CN0", "CN2")
        if not fin:
            tt(T.LA[:], T.CO[:, 16:24], T.CND[:, 0:8], A.subtract, "COc CN0", "LA")
            mm(T.ps5[:, 48:56], T.ONB[:], T.LA[:], True, True, "ONB LA", "ps5")
        tt(T.OF[:], T.CND[:], T.BSS[:, b0:b0 + 32], A.mult, "CN0 CN1 CN2 CN3 BSS", "OF")
        tt(T.OF[:], T.OF[:], T.DUM[:, 8:40], A.add, "OF DUM", "OF")
        cp(T.LS[:], T.OF[:], "OF", "LS")
        if not fin:
            m0 = 16 * t
            cp(T.MS[:, m0:m0 + 8], T.OF[:, 24:32], "OF", "MS")
            act(T.AQ[:], T.ps5[:, 48:56], AF.Copy, "", "AQ MSa", "ps5", accum_out=T.MS[:, m0 + 8:m0 + 9])
            send(nxt, T.ML[:, m0:m0 + 16], T.MS[:, m0:m0 + 16], "aM%d" % t, "MS MSa")
            if t == 2:
                cp(T.L8[:], T.OF[:, 24:32], "OF", "L8")
            arrives("aC%d" % t, "CL%d" % t)
            arrives("aZ%d" % t, "ZL%d" % t)
            arrives("aM%d" % t, "M%d" % t)
            zrep(T.ZL[:, 128 * t:128 * t + 128], "ZL%d" % t)
        tt(kwin().indirect(T.LS[:, 0:16]), T.VK[:], T.NR[:, 256 * t:256 * t + 256], A.add, "LS VKa VKb NR", "KN")
        cp(T.FX[:, 0:WN].indirect(T.LS[:, 8:24]), vf, "LS VF%d VFr" % t, "FX")
        cp(T.X[:].indirect(T.LS[:, 8:16]), zn, "LS " + znk, "X XL")
        if not fin:
            act(T.XW[:, a:a + 128], T.X[:, a:a + 128], AF.Copy, "X", "XW")

    def gap(t, s):
        if t == 0:
            constants3(s)
        elif s == 0:
            cp(T.AI[:, 0:1], T.ML[:, 16 * t - 8:16 * t - 7], "M%d" % (t - 1), "AI0")
            ts(T.AI[:, 1:2], T.AI[:, 0:1], 31, A.bitwise_and, rd="AI0", wr="AI1")
            ts(T.WAQ[:, 0:1], T.AI[:, 1:2], WT, A.mult, rd="AI1", wr="WA")
        if s == 0:
            cp(T.FX[:, 0:WN].indirect(T.LO[:, 8:24]), T.FVO[:], "LO FVO FVOr", "FX")

    fill(T.FVO[:, 128:256], float(NW), "FVOr")
    zrep(T.Z0[:], "Z0")
    convert(3, 2)
    out(0, lambda: start(0, T.BI[:], "BI"), lambda: convert(0, 1))
    fill(T.XW[:, lo[0]:lo[0] + 128], 4096.0, "XWp")
    for t in range(VIS):
        if t == 0:
            zz, zkey, wa, wkey = T.Z0[:], "Z0", WA0, "WA0"
        else:
            zz, zkey, wa, wkey = T.ZL[:, 128 * t - 128:128 * t], "ZL%d" % (t - 1), T.WAQ[:, 0:1], "WA"
        for s in range(ST):
            step(t, s, zz, zkey, wa, wkey, lambda: gap(t, s))
        seat(t, zz, zkey)
        if t == 2:
            dma("Y", "tb", T.TB[:], T.TT[0::16, 0:NW], rd="TT", wr="TB")
            send(prv, T.TBL[:], T.TB[:], "aTB", "TB")
            arrives("aTB", "TBL")
            dma("Y", "ot", T.OT[0::16, 0:NW], T.TBL[:], rd="TBL", wr="OT")
        if t < VIS - 1:
            fill(T.XW[:, lo[t + 1]:lo[t + 1] + 128], 4096.0, "XWp")
            out(t + 1, lambda: start(t + 1, T.TT[:].indirect(T.CL[:, 16 * t:16 * t + 8]), "TT TTd CL%d" % t))
    arrives("aB", "CLB")
    act(T.OR[:], T.ID[:].indirect(T.CL[:, 48:56]), AF.Copy, "ID CLB", "OR")
    dma("Y", "out", T.yz[:], T.ZN[:, 384:512], rd="ZN3")
    dma("S", "out", T.yk[:], T.KN[:, NB:NW], rd="KN")
    dma("Y", "out", T.yp[:], T.KN[0::16, 0:NB], rd="KN")
    dma("S", "out", T.yf[:], T.FX[0::16, NB:NW], rd="FX")
    dma("Y", "out", T.yx[:], T.X[:, NB:NW], rd="X")
    cp(T.OT[:].indirect(T.L8[:]), T.OR[:], "L8 OR", "OT")
    dma("Y", "out", T.yt[:], T.OT[0::16, 0:NW], rd="OT")
    for s in list(tot):
        need("G", s, tot[s])
